import numpy as np
import ml_dtypes


def mxq(x, axis, fmt="e4m3"):
    dtype, down = {"e4m3": (ml_dtypes.float8_e4m3fn, 7), "e5m2": (ml_dtypes.float8_e5m2, 14)}[fmt]
    v = np.moveaxis(np.asarray(x, np.float32).astype(ml_dtypes.bfloat16).astype(np.float64), axis, -1)
    blocks = v.reshape(v.shape[:-1] + (-1, 32))
    amax = np.abs(blocks).max(-1, keepdims=True)
    byte = np.maximum(np.where(amax > 0, np.frexp(amax)[1] - 1 + 127, 0) - down, 1)
    scale = np.exp2(byte - 127.0)
    codes = (blocks / scale).astype(np.float32).astype(dtype).astype(np.float64)
    return np.moveaxis((codes * scale).reshape(v.shape), -1, axis)


WIDE = False


def mx_kscale(k):
    if not WIDE:
        return np.ones(k)
    levels = np.array([10, -10, 5, -5, 0])
    if k % 512:
        return np.exp2(np.random.permutation(np.resize(levels, k // 32))).repeat(32)
    a = np.empty((k // 512, 16))
    for p in range(k // 512):
        a[p, :8] = np.random.permutation(np.resize(levels, 8))
        for g in range(8):
            far = levels[np.abs(levels - a[p, g]) >= 10]
            a[p, g + 8] = far[np.random.randint(len(far))]
    return np.exp2(a.ravel()).repeat(32)


def f64(x):
    return np.asarray(x).astype(np.float64)


def striped(idx):
    return np.tile(idx.reshape(-1, 16).T, (8, 1)).astype(np.uint16)


def unstriped(offs):
    return offs[:16].T.reshape(-1).astype(np.int64)


E2M1 = np.array([0.0, 0.5, 1.0, 1.5, 2.0, 3.0, 4.0, 6.0, -0.0, -0.5, -1.0, -1.5, -2.0, -3.0, -4.0, -6.0])


def pack_weight(w, fmt):
    k, n = w.shape
    w = f64(np.asarray(w, np.float32).astype(ml_dtypes.bfloat16)).reshape(k // 32, 32, n)
    amax = np.abs(w).max(1)
    if fmt == "e4m3":
        byte = np.frexp(amax)[1] - 1 + 127 - 7
    else:
        mant, ex = np.frexp(amax / 6.0)
        byte = np.where(mant > 0.5, ex, ex - 1) + 127
    byte = np.clip(np.where(amax > 0, byte, 1), 1, 254)
    scaled = (w * np.exp2(127.0 - byte)[:, None, :]).reshape(k, n).astype(np.float32)
    by_word = np.ascontiguousarray(scaled.reshape(k // 512, 128, 4, n).transpose(0, 1, 3, 2))
    if fmt == "e4m3":
        words = by_word.astype(ml_dtypes.float8_e4m3fn).view(np.uint8)
    else:
        c = by_word.astype(ml_dtypes.float4_e2m1fn).view(np.uint8) & 0xF
        words = (c[..., 0::2] | (c[..., 1::2] << 4)).reshape(k // 512, 128, 2 * n)
    return np.ascontiguousarray(words), np.ascontiguousarray(byte.astype(np.uint8).reshape(k // 512, 16, n))


def unpack_weight(words, scales, fmt):
    g, _, n = scales.shape
    words = np.ascontiguousarray(words).reshape(g, 128, n, -1)
    if fmt == "e4m3":
        vals = words.view(ml_dtypes.float8_e4m3fn).astype(np.float64)
    else:
        nib = np.empty((g, 128, n, 4), np.uint8)
        nib[..., 0::2] = words & 0xF
        nib[..., 1::2] = words >> 4
        vals = E2M1[nib]
    vals = vals * np.repeat(np.exp2(scales.astype(np.float64) - 127.0), 8, axis=1)[..., None]
    return vals.transpose(0, 1, 3, 2).reshape(g * 512, n)


def relu2(v):
    return np.maximum(v, 0.0) ** 2


K, T, E, C, N = 1024, 1024, 8, 128, 256


def by_expert(wq, xq):
    return np.concatenate([wq[e].T @ xq[:, e * C:(e + 1) * C] for e in range(E)], axis=1)


def setup_inputs():
    n = np.random.standard_normal
    s = mx_kscale(K)[:, None]
    w = [pack_weight(m, "e2m1") for m in n((E + 1, K, N)) / np.sqrt(K) / s[None]]
    return {
        "xT": (n((K, T)) * s).astype(np.float32),
        "w_words": np.stack([m[0] for m in w]),
        "w_scales": np.stack([m[1] for m in w]),
        "b": (0.3 * n((N, E + 1))).astype(np.float32),
        "gate": np.tile(np.random.uniform(0.2, 1.0, E * C), (N, 1)).astype(np.float32),
        "offs": striped(np.random.permutation(T)[:E * C]),
    }


def reference(xT, w_words, w_scales, b, gate, offs):
    idx = unstriped(offs)
    w = np.stack([unpack_weight(w_words[e], w_scales[e], "e2m1") for e in range(E + 1)])
    wq = w
    xs = mxq(f64(xT), 0, "e4m3")
    ys = relu2((wq[E].T @ xs) + f64(b)[:, E:])
    xq = mxq(f64(xT)[:, idx], 0, "e4m3")
    y = by_expert(w, xq)
    y = relu2(y + np.repeat(f64(b)[:, :E], C, axis=1))
    out = ys
    out[:, idx] += f64(gate) * y
    return out

@@ -1,0 +1,198 @@
+from contextlib import ExitStack
+
+import concourse.mybir as mybir
+
+K, T, E, C, N = 1024, 1024, 8, 128, 256
+FLOPS = 2 * 2 * K * T * N
+
+F32 = mybir.dt.float32
+BF16 = mybir.dt.bfloat16
+U32 = mybir.dt.uint32
+I32 = mybir.dt.int32
+U16 = mybir.dt.uint16
+U8 = mybir.dt.uint8
+FP8X4 = mybir.dt.float8_e4m3fn_x4
+FP4X4 = mybir.dt.float4_e2m1fn_x4
+
+ADD = mybir.AluOpType.add
+MULT = mybir.AluOpType.mult
+RELU = mybir.ActivationFunctionType.Relu
+SQUARE = mybir.ActivationFunctionType.Square
+
+P = 128
+A = K // 512
+Q = 256
+NQ = T // Q
+
+
+def tile_moe_shr_lin_relu2_kernel(tc, xT, w_words, w_scales, b, gate, offs, out):
+    nc = tc.nc
+    with ExitStack() as ctx:
+        held = ctx.enter_context(tc.tile_pool(name="held", bufs=1))
+        work = ctx.enter_context(tc.tile_pool(name="work", bufs=3))
+        psum = ctx.enter_context(tc.psum_pool(name="psum", bufs=1))
+
+        offsets = held.tile([P, T // 16], U16, name="offsets")
+
+        dummy = held.tile([P, 1], F32, name="dummy")
+        nc.vector.memset(dummy[:], 0.0)
+        nc.scalar.activation(dummy[:], dummy[:], RELU)
+
+        planes = held.tile([P, (E + 1) * A, N], U8, name="planes", align_bytes=64)
+        nc.gpsimd.memset(planes[:].bitcast(I32), 0)
+
+        x_view = xT.rearrange("(a p u e) n -> a u p e n", p=P, u=2, e=2)
+        raws = {}
+
+        def load_x(a, u):
+            for s in range(2):
+                raw = held.tile([P, 2, 512], F32, name=f"raw{a}{u}{s}", align_bytes=64)
+                nc.sync.dma_start(raw[:], x_view[a, u][:, :, 512 * s : 512 * s + 512])
+                raws[a, u, s] = raw
+
+        w_view = w_words.bitcast(I32)
+        w_at = {}
+
+        def load_w(first, count):
+            tile = held.tile([P, count * A, 2 * N], U8, name=f"words{first}", align_bytes=64)
+            nc.sync.dma_start(tile[:].bitcast(I32), w_view[first : first + count].rearrange("e a p c -> p (e a) c"))
+            for i in range(count):
+                w_at[first + i] = (tile, i * A)
+
+        s_view = w_scales.bitcast(I32)
+        load_x(0, 0)
+        nc.sync.dma_start(offsets[:], offs)
+        load_x(0, 1)
+        load_x(1, 0)
+        for quad in range(4):
+            nc.sync.dma_start(
+                planes[32 * quad : 32 * quad + 4].bitcast(I32),
+                s_view[:, :, 4 * quad : 4 * quad + 4, :].rearrange("e a q n -> q (e a) n"),
+            )
+        load_x(1, 1)
+        load_w(8, 1)
+        load_w(0, 2)
+        bias = held.tile([P, 2, E + 1], F32, name="bias")
+        nc.sync.dma_start(bias[:], b.rearrange("(h p) e -> p h e", p=P))
+        gates = held.tile([P, T], F32, name="gates")
+        nc.sync.dma_start(gates[:, 0:512], gate[0:P, 0:512])
+        load_w(2, 2)
+        load_w(4, 4)
+        nc.sync.dma_start(gates[:, 512:T], gate[0:P, 512:T])
+
+        copies = {"S": nc.scalar.copy, "V": nc.vector.tensor_copy, "G": nc.gpsimd.tensor_copy}
+        pairs = {}
+
+        def cast(a, u, parts):
+            pair = held.tile([P, T, 2], BF16, name=f"pair{a}{u}", align_bytes=64)
+            pairs[a, u] = pair
+            for engine, first, last in parts:
+                at = first % 512
+                copies[engine](pair[:, first:last, :], raws[a, u, first // 512][:, :, at : at + last - first].rearrange("p e n -> p n e"))
+
+        def gather(a, u, dst, first, count):
+            window = pairs[a, u][:].rearrange("p n e -> p (n e)").bitcast(U32)
+            idx = offsets[:, first // 16 : (first + count) // 16]
+            nc.vector.tensor_copy(dst.rearrange("p (n u) -> p n u", u=2)[:, :, u], window.indirect(idx))
+
+        codes = {}
+        scales = {}
+
+        def quantize(a, i, words, first, count):
+            nc.vector.quantize_mx(
+                out=codes[a, i][:, first : first + count].bitcast(FP8X4),
+                scales=scales[a, i][:, first : first + count],
+                in_=words[:, 2 * first : 2 * (first + count)].bitcast(BF16),
+            )
+
+        for a in range(A):
+            for i in range(2):
+                scales[a, i] = held.tile([P, 512], U8, name=f"scales{a}{i}", align_bytes=64)
+                if (a, i) != (0, 1):
+                    codes[a, i] = held.tile([P, 512], U32, name=f"codes{a}{i}", align_bytes=64)[:]
+        words0 = [held.tile([P, 1024], U32, name=f"words0_{i}", align_bytes=64) for i in range(2)]
+
+        cast(0, 0, [("S", 0, 512), ("V", 512, 896), ("S", 896, 1024)])
+        for i in range(2):
+            gather(0, 0, words0[i][:], 512 * i, 512)
+        cast(0, 1, [("S", 0, 512), ("S", 512, 768), ("G", 768, 1024)])
+        for i in range(2):
+            gather(0, 1, words0[i][:], 512 * i, 512)
+        cast(1, 0, [("S", 0, 512), ("S", 512, 1024)])
+        early = held.tile([P, 1024], U32, name="turns", align_bytes=64)
+        gather(1, 0, early[:], 0, 512)
+        quantize(0, 0, words0[0][:], 0, 512)
+        cast(1, 1, [("S", 0, 512), ("S", 512, 1024)])
+        for q in range(2):
+            gather(1, 1, early[:, 512 * q : 512 * q + 512], Q * q, Q)
+        for q in range(2):
+            quantize(1, 0, early[:], Q * q, Q)
+        late = held.tile([P, 1024], U32, name="turns", align_bytes=64)
+        codes[0, 1] = held.tile([P, 512], U32, name="raw111", align_bytes=64)[:]
+        gather(1, 0, late[:], 512, 512)
+        gather(1, 1, late[:], 512, 512)
+        quantize(0, 1, words0[1][:], 0, 512)
+        quantize(1, 1, late[:], 0, 512)
+
+        windows = [held.tile([P, T], F32, name=f"window{h}") for h in range(2)]
+
+        def product(out_ap, e, h, i, first, count):
+            tile, at = w_at[e]
+            for a in range(A):
+                nc.tensor.matmul_mx(
+                    out=out_ap,
+                    lhsT=tile[:, at + a, N * h : N * h + N].bitcast(FP4X4),
+                    lhsT_scale=planes[:, e * A + a, P * h : P * h + P],
+                    rhs=codes[a, i][:, first : first + count].bitcast(FP8X4),
+                    rhs_scale=scales[a, i][:, first : first + count],
+                    start=(a == 0),
+                    stop=(a == A - 1),
+                )
+
+        def combine(h, first, sq_y, sq_s, engines):
+            t = work.tile([P, Q], F32, name="t")
+            o = work.tile([P, Q], F32, name="o")
+            engines[0].tensor_tensor(t[:], sq_y, gates[:, first : first + Q], MULT)
+            engines[1].tensor_tensor(o[:], t[:], sq_s, ADD)
+            nc.vector.tensor_copy(windows[h][:].indirect(offsets[:, first // 16 : (first + Q) // 16]), o[:])
+
+        def small_unit(h, q, engines):
+            bank = psum.tile([P, 4, C], F32, name=f"bank{h}{q}")
+            for j in range(2):
+                product(bank[:, j, :], 2 * q + j, h, 0, Q * q + C * j, C)
+            for j in range(2):
+                product(bank[:, 2 + j, :], E, h, 0, Q * q + C * j, C)
+            r = work.tile([P, 4, C], F32, name="r")
+            for j in range(2):
+                e = 2 * q + j
+                nc.scalar.activation(r[:, j, :], bank[:, j, :], RELU, bias=bias[:, h, e : e + 1])
+            nc.scalar.activation(r[:, 2:4, :], bank[:, 2:4, :], RELU, bias=bias[:, h, E : E + 1])
+            sq = work.tile([P, 4 * C], F32, name="sq")
+            nc.scalar.activation(sq[:], r[:].rearrange("p j c -> p (j c)"), SQUARE)
+            combine(h, Q * q, sq[:, 0:Q], sq[:, Q : 2 * Q], engines)
+
+        def big_unit(h, engines):
+            y = psum.tile([P, 4, C], F32, name=f"bank_y{h}")
+            s = psum.tile([P, 4 * C], F32, name=f"bank_s{h}")
+            for j in range(4):
+                product(y[:, j, :], 4 + j, h, 1, C * j, C)
+            product(s[:], E, h, 1, 0, 512)
+            r = work.tile([P, 8, C], F32, name="r_big")
+            sq = work.tile([P, 8 * C], F32, name="sq_big")
+            for j in range(4):
+                e = 4 + j
+                nc.scalar.activation(r[:, j, :], y[:, j, :], RELU, bias=bias[:, h, e : e + 1])
+            nc.scalar.activation(sq[:, 0:512], r[:, 0:4, :].rearrange("p j c -> p (j c)"), SQUARE)
+            nc.scalar.activation(r[:, 4:8, :].rearrange("p j c -> p (j c)"), s[:], RELU, bias=bias[:, h, E : E + 1])
+            nc.scalar.activation(sq[:, 512:1024], r[:, 4:8, :].rearrange("p j c -> p (j c)"), SQUARE)
+            for i in range(2):
+                combine(h, 512 + Q * i, sq[:, Q * i : Q * i + Q], sq[:, 512 + Q * i : 512 + Q * i + Q], engines[i])
+
+        V, G = nc.vector, nc.gpsimd
+        small_unit(0, 0, (V, V))
+        small_unit(1, 0, (G, G))
+        small_unit(0, 1, (G, G))
+        small_unit(1, 1, (G, G))
+        for h in range(2):
+            big_unit(h, [(G, G), (G, G)])
+            nc.sync.dma_start(out[P * h : P * h + P, :], windows[h][:])

@@ -29,7 +29,7 @@ def tile_moe_shr_lin_relu2_kernel(tc, xT, w_words, w_scales, b, gate, offs, out)
     nc = tc.nc
     with ExitStack() as ctx:
         held = ctx.enter_context(tc.tile_pool(name="held", bufs=1))
-        work = ctx.enter_context(tc.tile_pool(name="work", bufs=3))
+        ring = ctx.enter_context(tc.tile_pool(name="ring", bufs=2))
         psum = ctx.enter_context(tc.psum_pool(name="psum", bufs=1))
 
         offsets = held.tile([P, T // 16], U16, name="offsets")
@@ -38,8 +38,16 @@ def tile_moe_shr_lin_relu2_kernel(tc, xT, w_words, w_scales, b, gate, offs, out)
         nc.vector.memset(dummy[:], 0.0)
         nc.scalar.activation(dummy[:], dummy[:], RELU)
 
-        planes = held.tile([P, (E + 1) * A, N], U8, name="planes", align_bytes=64)
-        nc.gpsimd.memset(planes[:].bitcast(I32), 0)
+        firsts = [T - Q * (q + 1) for q in range(NQ)]
+
+        w_at = {}
+        s_at = {}
+        planes = {}
+        for first, count in ((6, 3), (0, 6)):
+            planes[first] = held.tile([P, count * A, N], U8, name=f"planes{first}", align_bytes=64)
+            nc.gpsimd.memset(planes[first][:].bitcast(I32), 0)
+            for i in range(count):
+                s_at[first + i] = (planes[first], i * A)
 
         x_view = xT.rearrange("(a p u e) n -> a u p e n", p=P, u=2, e=2)
         raws = {}
@@ -51,7 +59,7 @@ def tile_moe_shr_lin_relu2_kernel(tc, xT, w_words, w_scales, b, gate, offs, out)
                 raws[a, u, s] = raw
 
         w_view = w_words.bitcast(I32)
-        w_at = {}
+        s_view = w_scales.bitcast(I32)
 
         def load_w(first, count):
             tile = held.tile([P, count * A, 2 * N], U8, name=f"words{first}", align_bytes=64)
@@ -59,28 +67,34 @@ def tile_moe_shr_lin_relu2_kernel(tc, xT, w_words, w_scales, b, gate, offs, out)
             for i in range(count):
                 w_at[first + i] = (tile, i * A)
 
-        s_view = w_scales.bitcast(I32)
+        def load_scales(first, count):
+            for quad in range(4):
+                nc.sync.dma_start(
+                    planes[first][32 * quad : 32 * quad + 4].bitcast(I32),
+                    s_view[first : first + count, :, 4 * quad : 4 * quad + 4, :].rearrange("e a q n -> q (e a) n"),
+                )
+
+        bias = held.tile([P, 2, E + 1], F32, name="bias")
+        gates = [held.tile([P, 512], F32, name=f"gates{i}") for i in range(2)]
+
         load_x(0, 0)
         nc.sync.dma_start(offsets[:], offs)
         load_x(0, 1)
         load_x(1, 0)
-        for quad in range(4):
-            nc.sync.dma_start(
-                planes[32 * quad : 32 * quad + 4].bitcast(I32),
-                s_view[:, :, 4 * quad : 4 * quad + 4, :].rearrange("e a q n -> q (e a) n"),
-            )
         load_x(1, 1)
-        load_w(8, 1)
-        load_w(0, 2)
-        bias = held.tile([P, 2, E + 1], F32, name="bias")
+        load_scales(6, 3)
+        load_w(6, 3)
         nc.sync.dma_start(bias[:], b.rearrange("(h p) e -> p h e", p=P))
-        gates = held.tile([P, T], F32, name="gates")
-        nc.sync.dma_start(gates[:, 0:512], gate[0:P, 0:512])
-        load_w(2, 2)
-        load_w(4, 4)
-        nc.sync.dma_start(gates[:, 512:T], gate[0:P, 512:T])
+        nc.sync.dma_start(gates[1][:], gate[0:P, 512:T])
+        load_w(4, 2)
+        load_scales(0, 6)
+        load_w(0, 4)
+        nc.sync.dma_start(gates[0][:], gate[0:P, 0:512])
 
-        copies = {"S": nc.scalar.copy, "V": nc.vector.tensor_copy, "G": nc.gpsimd.tensor_copy}
+        def gpsimd_cast(dst, src):
+            nc.gpsimd.tensor_scalar(dst, src, 1.0, 0.0, MULT, ADD)
+
+        copies = {"S": nc.scalar.copy, "V": nc.vector.tensor_copy, "G": gpsimd_cast}
         pairs = {}
 
         def cast(a, u, parts):
@@ -92,107 +106,141 @@ def tile_moe_shr_lin_relu2_kernel(tc, xT, w_words, w_scales, b, gate, offs, out)
 
         def gather(a, u, dst, first, count):
             window = pairs[a, u][:].rearrange("p n e -> p (n e)").bitcast(U32)
-            idx = offsets[:, first // 16 : (first + count) // 16]
-            nc.vector.tensor_copy(dst.rearrange("p (n u) -> p n u", u=2)[:, :, u], window.indirect(idx))
+            nc.vector.tensor_copy(dst, window.indirect(offsets[:, first // 16 : (first + count) // 16]))
+
+        def weave(dst, src):
+            nc.scalar.copy(dst.rearrange("p (n u) -> p n u", u=2), src.rearrange("p u n -> p n u"))
 
         codes = {}
         scales = {}
 
-        def quantize(a, i, words, first, count):
-            nc.vector.quantize_mx(
-                out=codes[a, i][:, first : first + count].bitcast(FP8X4),
-                scales=scales[a, i][:, first : first + count],
-                in_=words[:, 2 * first : 2 * (first + count)].bitcast(BF16),
-            )
+        shared = [("S", 0, 128), ("G", 128, 512), ("S", 512, 832), ("G", 832, 1024)]
 
-        for a in range(A):
-            for i in range(2):
-                scales[a, i] = held.tile([P, 512], U8, name=f"scales{a}{i}", align_bytes=64)
-                if (a, i) != (0, 1):
-                    codes[a, i] = held.tile([P, 512], U32, name=f"codes{a}{i}", align_bytes=64)[:]
-        words0 = [held.tile([P, 1024], U32, name=f"words0_{i}", align_bytes=64) for i in range(2)]
+        stage0 = held.tile([P, 2, T], U32, name="stage0", align_bytes=64)
+        cast(0, 0, [("S", 0, 256), ("V", 256, 512), ("S", 512, 672), ("V", 672, 1024)])
+        for first in (512, 0):
+            gather(0, 0, stage0[:, 0, first : first + 512], first, 512)
+        cast(0, 1, shared)
+        for first, count in ((3 * Q, Q), (2 * Q, Q), (0, 2 * Q)):
+            gather(0, 1, stage0[:, 1, first : first + count], first, count)
 
-        cast(0, 0, [("S", 0, 512), ("V", 512, 896), ("S", 896, 1024)])
-        for i in range(2):
-            gather(0, 0, words0[i][:], 512 * i, 512)
-        cast(0, 1, [("S", 0, 512), ("S", 512, 768), ("G", 768, 1024)])
-        for i in range(2):
-            gather(0, 1, words0[i][:], 512 * i, 512)
-        cast(1, 0, [("S", 0, 512), ("S", 512, 1024)])
-        early = held.tile([P, 1024], U32, name="turns", align_bytes=64)
-        gather(1, 0, early[:], 0, 512)
-        quantize(0, 0, words0[0][:], 0, 512)
-        cast(1, 1, [("S", 0, 512), ("S", 512, 1024)])
-        for q in range(2):
-            gather(1, 1, early[:, 512 * q : 512 * q + 512], Q * q, Q)
-        for q in range(2):
-            quantize(1, 0, early[:], Q * q, Q)
-        late = held.tile([P, 1024], U32, name="turns", align_bytes=64)
-        codes[0, 1] = held.tile([P, 512], U32, name="raw111", align_bytes=64)[:]
-        gather(1, 0, late[:], 512, 512)
-        gather(1, 1, late[:], 512, 512)
-        quantize(0, 1, words0[1][:], 0, 512)
-        quantize(1, 1, late[:], 0, 512)
+        woven0 = {}
 
-        windows = [held.tile([P, T], F32, name=f"window{h}") for h in range(2)]
+        def weave0(units, name):
+            tile = held.tile([P, 2 * Q * len(units)], U32, name=name, align_bytes=64)
+            for i, q in enumerate(units):
+                woven0[q] = tile[:, 2 * Q * i : 2 * Q * (i + 1)]
+                weave(woven0[q], stage0[:, :, firsts[q] : firsts[q] + Q])
 
-        def product(out_ap, e, h, i, first, count):
-            tile, at = w_at[e]
+        spans = [(7 * C, C), (6 * C, C), (2 * Q, Q), (0, 2 * Q)]
+        woven1 = {}
+
+        def gather1(u, i):
+            gather(1, u, woven1[i][:, :, u], *spans[i])
+
+        cast(1, 0, [("G", 0, 512), ("S", 512, 1024)])
+        weave0([0], "woven00")
+        for i in range(3):
+            woven1[i] = held.tile([P, spans[i][1], 2], U32, name=f"woven1_{i}", align_bytes=64)
+            gather1(0, i)
+        weave0([1], "raw101")
+        cast(1, 1, [("S", 0, 256), ("G", 256, 512), ("S", 512, 688), ("V", 688, 1024)])
+        weave0([2, 3], "raw110")
+        woven1[3] = held.tile([P, spans[3][1], 2], U32, name="stage0", align_bytes=64)
+        codes0 = held.tile([P, T], U32, name="raw111", align_bytes=64)
+
+        def quantize(a, first, count, words):
+            code = codes0[:, first : first + count] if a == 0 else held.tile([P, count], U32, name=f"codes1_{first}", align_bytes=64)[:]
+            scale = held.tile([P, count], U8, name=f"scales{a}_{first}", align_bytes=64)
+            nc.vector.quantize_mx(out=code.bitcast(FP8X4), scales=scale[:], in_=words.bitcast(BF16))
+            for at in range(0, count, C):
+                codes[a, (first + at) // C] = code[:, at : at + C]
+                scales[a, (first + at) // C] = scale[:, at : at + C]
+
+        def quantize1(i):
+            quantize(1, *spans[i], woven1[i][:].rearrange("p n u -> p (n u)"))
+
+        gather1(1, 0)
+        quantize(0, firsts[0], Q, woven0[0])
+        quantize1(0)
+        gather1(1, 1)
+        quantize(0, firsts[1], Q, woven0[1])
+        quantize1(1)
+        gather1(1, 2)
+        quantize(0, firsts[2], Q, woven0[2])
+        quantize(0, firsts[3], Q, woven0[3])
+        quantize1(2)
+        gather1(0, 3)
+        gather1(1, 3)
+        quantize1(3)
+
+        windows = [held.tile([P, T], F32, name=name, align_bytes=64) for name in ("stage0", "pair11")]
+
+        def product(out_ap, e, h, block):
+            words, at = w_at[e]
+            plane, at_s = s_at[e]
             for a in range(A):
                 nc.tensor.matmul_mx(
                     out=out_ap,
-                    lhsT=tile[:, at + a, N * h : N * h + N].bitcast(FP4X4),
-                    lhsT_scale=planes[:, e * A + a, P * h : P * h + P],
-                    rhs=codes[a, i][:, first : first + count].bitcast(FP8X4),
-                    rhs_scale=scales[a, i][:, first : first + count],
+                    lhsT=words[:, at + a, N * h : N * h + N].bitcast(FP4X4),
+                    lhsT_scale=plane[:, at_s + a, P * h : P * h + P],
+                    rhs=codes[a, block].bitcast(FP8X4),
+                    rhs_scale=scales[a, block],
                     start=(a == 0),
                     stop=(a == A - 1),
                 )
 
-        def combine(h, first, sq_y, sq_s, engines):
-            t = work.tile([P, Q], F32, name="t")
-            o = work.tile([P, Q], F32, name="o")
-            engines[0].tensor_tensor(t[:], sq_y, gates[:, first : first + Q], MULT)
-            engines[1].tensor_tensor(o[:], t[:], sq_s, ADD)
-            nc.vector.tensor_copy(windows[h][:].indirect(offsets[:, first // 16 : (first + Q) // 16]), o[:])
+        def unit(first, count, banks, groups, fused):
+            blocks = range(first // C, (first + count) // C)
+            y = [psum.tile([P, count], F32, name=f"bank{banks + h}") for h in range(2)]
+            s = [psum.tile([P, count], F32, name=f"bank{banks + 2 + h}") for h in range(2)]
+            weights = gates[first // 512][:, first % 512 : first % 512 + count]
+            places = [windows[h][:].indirect(offsets[:, first // 16 : (first + count) // 16]) for h in range(2)]
+            for group in groups:
+                n = len(group)
+                tag = f"{first}_{group[0]}"
+                for h in group:
+                    for j, e in enumerate(blocks):
+                        product(y[h][:, C * j : C * j + C], e, h, e)
+                for h in group:
+                    for j, e in enumerate(blocks):
+                        product(s[h][:, C * j : C * j + C], E, h, e)
+                r_y = ring.tile([P, n, count], F32, name="r")
+                sq_y = held.tile([P, n, count], F32, name=f"sq_y{tag}")
+                t = held.tile([P, n, count], F32, name=f"t{tag}")
+                for i, h in enumerate(group):
+                    for j, e in enumerate(blocks):
+                        nc.scalar.activation(r_y[:, i, C * j : C * j + C], y[h][:, C * j : C * j + C], RELU, bias=bias[:, h, e : e + 1])
+                nc.scalar.activation(sq_y[:], r_y[:], SQUARE)
+                nc.gpsimd.tensor_tensor(t[:], sq_y[:], weights.unsqueeze(1).to_broadcast([P, n, count]), MULT)
+                if count == C:
+                    r_s = ring.tile([P, n, count], F32, name="r")
+                    sq_s = held.tile([P, n, count], F32, name=f"sq_s{tag}")
+                    o = held.tile([P, n, count], F32, name=f"o{tag}")
+                    for i, h in enumerate(group):
+                        nc.scalar.activation(r_s[:, i, :], s[h][:], RELU, bias=bias[:, h, E : E + 1])
+                    nc.scalar.activation(sq_s[:], r_s[:], SQUARE)
+                    nc.gpsimd.tensor_tensor(o[:], t[:], sq_s[:], ADD)
+                    for i, h in enumerate(group):
+                        nc.vector.tensor_copy(places[h], o[:, i, :])
+                    continue
+                for i, h in enumerate(group):
+                    r_s = ring.tile([P, count], F32, name="r")
+                    sq_s = held.tile([P, count], F32, name=f"sq_s{first}_{h}")
+                    nc.scalar.activation(r_s[:], s[h][:], RELU, bias=bias[:, h, E : E + 1])
+                    nc.scalar.activation(sq_s[:], r_s[:], SQUARE)
+                    if h in fused:
+                        nc.vector.tensor_tensor(places[h], t[:, i, :], sq_s[:], ADD)
+                    else:
+                        o = held.tile([P, count], F32, name=f"o{first}_{h}")
+                        nc.gpsimd.tensor_tensor(o[:], t[:, i, :], sq_s[:], ADD)
+                        nc.vector.tensor_copy(places[h], o[:])
 
-        def small_unit(h, q, engines):
-            bank = psum.tile([P, 4, C], F32, name=f"bank{h}{q}")
-            for j in range(2):
-                product(bank[:, j, :], 2 * q + j, h, 0, Q * q + C * j, C)
-            for j in range(2):
-                product(bank[:, 2 + j, :], E, h, 0, Q * q + C * j, C)
-            r = work.tile([P, 4, C], F32, name="r")
-            for j in range(2):
-                e = 2 * q + j
-                nc.scalar.activation(r[:, j, :], bank[:, j, :], RELU, bias=bias[:, h, e : e + 1])
-            nc.scalar.activation(r[:, 2:4, :], bank[:, 2:4, :], RELU, bias=bias[:, h, E : E + 1])
-            sq = work.tile([P, 4 * C], F32, name="sq")
-            nc.scalar.activation(sq[:], r[:].rearrange("p j c -> p (j c)"), SQUARE)
-            combine(h, Q * q, sq[:, 0:Q], sq[:, Q : 2 * Q], engines)
-
-        def big_unit(h, engines):
-            y = psum.tile([P, 4, C], F32, name=f"bank_y{h}")
-            s = psum.tile([P, 4 * C], F32, name=f"bank_s{h}")
-            for j in range(4):
-                product(y[:, j, :], 4 + j, h, 1, C * j, C)
-            product(s[:], E, h, 1, 0, 512)
-            r = work.tile([P, 8, C], F32, name="r_big")
-            sq = work.tile([P, 8 * C], F32, name="sq_big")
-            for j in range(4):
-                e = 4 + j
-                nc.scalar.activation(r[:, j, :], y[:, j, :], RELU, bias=bias[:, h, e : e + 1])
-            nc.scalar.activation(sq[:, 0:512], r[:, 0:4, :].rearrange("p j c -> p (j c)"), SQUARE)
-            nc.scalar.activation(r[:, 4:8, :].rearrange("p j c -> p (j c)"), s[:], RELU, bias=bias[:, h, E : E + 1])
-            nc.scalar.activation(sq[:, 512:1024], r[:, 4:8, :].rearrange("p j c -> p (j c)"), SQUARE)
-            for i in range(2):
-                combine(h, 512 + Q * i, sq[:, Q * i : Q * i + Q], sq[:, 512 + Q * i : 512 + Q * i + Q], engines[i])
-
-        V, G = nc.vector, nc.gpsimd
-        small_unit(0, 0, (V, V))
-        small_unit(1, 0, (G, G))
-        small_unit(0, 1, (G, G))
-        small_unit(1, 1, (G, G))
+        both = [(0, 1)]
+        unit(*spans[0], 0, both, ())
+        unit(*spans[1], 4, both, ())
+        unit(*spans[2], 0, both, ())
+        unit(Q, Q, 0, both, (1,))
+        unit(0, Q, 0, both, (0, 1))
         for h in range(2):
-            big_unit(h, [(G, G), (G, G)])
             nc.sync.dma_start(out[P * h : P * h + P, :], windows[h][:])

@@ -132,21 +132,29 @@ def tile_moe_shr_lin_relu2_kernel(tc, xT, w_words, w_scales, b, gate, offs, out)
                 woven0[q] = tile[:, 2 * Q * i : 2 * Q * (i + 1)]
                 weave(woven0[q], stage0[:, :, firsts[q] : firsts[q] + Q])
 
-        spans = [(7 * C, C), (6 * C, C), (2 * Q, Q), (0, 2 * Q)]
+        spans = [(7 * C, C), (6 * C, C), (2 * Q, Q), (Q, Q), (0, Q)]
         woven1 = {}
+        stage1 = {}
 
         def gather1(u, i):
-            gather(1, u, woven1[i][:, :, u], *spans[i])
+            gather(1, u, woven1[i][:, :, u] if i < 2 else stage1[i][:, u, :], *spans[i])
+
+        def weave1(i, name):
+            woven1[i] = held.tile([P, Q, 2], U32, name=name, align_bytes=64)
+            weave(woven1[i][:].rearrange("p n u -> p (n u)"), stage1[i])
 
         cast(1, 0, [("G", 0, 512), ("S", 512, 1024)])
         weave0([0], "woven00")
-        for i in range(3):
-            woven1[i] = held.tile([P, spans[i][1], 2], U32, name=f"woven1_{i}", align_bytes=64)
+        for i in range(2):
+            woven1[i] = held.tile([P, C, 2], U32, name=f"woven1_{i}", align_bytes=64)
+            gather1(0, i)
+        for i in (2, 3):
+            stage1[i] = held.tile([P, 2, Q], U32, name=f"stage1_{i}", align_bytes=64)[:]
             gather1(0, i)
         weave0([1], "raw101")
-        cast(1, 1, [("S", 0, 256), ("G", 256, 512), ("S", 512, 688), ("V", 688, 1024)])
+        cast(1, 1, [("S", 0, 256), ("G", 256, 512), ("S", 512, 832), ("G", 832, 1024)])
         weave0([2, 3], "raw110")
-        woven1[3] = held.tile([P, spans[3][1], 2], U32, name="stage0", align_bytes=64)
+        stage1[4] = held.tile([P, 2, Q], U32, name="stage0", align_bytes=64)[:]
         codes0 = held.tile([P, T], U32, name="raw111", align_bytes=64)
 
         def quantize(a, first, count, words):
@@ -163,18 +171,19 @@ def tile_moe_shr_lin_relu2_kernel(tc, xT, w_words, w_scales, b, gate, offs, out)
         gather1(1, 0)
         quantize(0, firsts[0], Q, woven0[0])
         quantize1(0)
+        gather1(1, 2)
+        weave1(2, "woven1_2")
         gather1(1, 1)
         quantize(0, firsts[1], Q, woven0[1])
         quantize1(1)
-        gather1(1, 2)
         quantize(0, firsts[2], Q, woven0[2])
         quantize(0, firsts[3], Q, woven0[3])
         quantize1(2)
-        gather1(0, 3)
         gather1(1, 3)
-        quantize1(3)
+        gather1(0, 4)
+        gather1(1, 4)
 
-        windows = [held.tile([P, T], F32, name=name, align_bytes=64) for name in ("stage0", "pair11")]
+        windows = [held.tile([P, T], F32, name=name, align_bytes=64) for name in ("pair10", "pair11")]
 
         def product(out_ap, e, h, block):
             words, at = w_at[e]
@@ -206,7 +215,7 @@ def tile_moe_shr_lin_relu2_kernel(tc, xT, w_words, w_scales, b, gate, offs, out)
                     for j, e in enumerate(blocks):
                         product(s[h][:, C * j : C * j + C], E, h, e)
                 r_y = ring.tile([P, n, count], F32, name="r")
-                sq_y = held.tile([P, n, count], F32, name=f"sq_y{tag}")
+                sq_y = held.tile([P, n, count], F32, name=f"sq_y{tag}", align_bytes=64)
                 t = held.tile([P, n, count], F32, name=f"t{tag}")
                 for i, h in enumerate(group):
                     for j, e in enumerate(blocks):
@@ -215,7 +224,7 @@ def tile_moe_shr_lin_relu2_kernel(tc, xT, w_words, w_scales, b, gate, offs, out)
                 nc.gpsimd.tensor_tensor(t[:], sq_y[:], weights.unsqueeze(1).to_broadcast([P, n, count]), MULT)
                 if count == C:
                     r_s = ring.tile([P, n, count], F32, name="r")
-                    sq_s = held.tile([P, n, count], F32, name=f"sq_s{tag}")
+                    sq_s = held.tile([P, n, count], F32, name=f"sq_s{tag}", align_bytes=64)
                     o = held.tile([P, n, count], F32, name=f"o{tag}")
                     for i, h in enumerate(group):
                         nc.scalar.activation(r_s[:, i, :], s[h][:], RELU, bias=bias[:, h, E : E + 1])
@@ -239,7 +248,10 @@ def tile_moe_shr_lin_relu2_kernel(tc, xT, w_words, w_scales, b, gate, offs, out)
         both = [(0, 1)]
         unit(*spans[0], 0, both, ())
         unit(*spans[1], 4, both, ())
-        unit(*spans[2], 0, both, ())
+        for i, name in ((3, f"sq_s{7 * C}_0"), (4, f"sq_y{6 * C}_0")):
+            weave1(i, name)
+            quantize1(i)
+        unit(*spans[2], 0, [(0,), (1,)], ())
         unit(Q, Q, 0, both, (1,))
         unit(0, Q, 0, both, (0, 1))
         for h in range(2):

@@ -143,18 +143,17 @@ def tile_moe_shr_lin_relu2_kernel(tc, xT, w_words, w_scales, b, gate, offs, out)
             woven1[i] = held.tile([P, Q, 2], U32, name=name, align_bytes=64)
             weave(woven1[i][:].rearrange("p n u -> p (n u)"), stage1[i])
 
-        cast(1, 0, [("G", 0, 512), ("S", 512, 1024)])
+        cast(1, 0, shared)
         weave0([0], "woven00")
         for i in range(2):
             woven1[i] = held.tile([P, C, 2], U32, name=f"woven1_{i}", align_bytes=64)
             gather1(0, i)
-        for i in (2, 3):
+        for i in (2, 3, 4):
             stage1[i] = held.tile([P, 2, Q], U32, name=f"stage1_{i}", align_bytes=64)[:]
             gather1(0, i)
         weave0([1], "raw101")
         cast(1, 1, [("S", 0, 256), ("G", 256, 512), ("S", 512, 832), ("G", 832, 1024)])
         weave0([2, 3], "raw110")
-        stage1[4] = held.tile([P, 2, Q], U32, name="stage0", align_bytes=64)[:]
         codes0 = held.tile([P, T], U32, name="raw111", align_bytes=64)
 
         def quantize(a, first, count, words):
@@ -180,7 +179,6 @@ def tile_moe_shr_lin_relu2_kernel(tc, xT, w_words, w_scales, b, gate, offs, out)
         quantize(0, firsts[3], Q, woven0[3])
         quantize1(2)
         gather1(1, 3)
-        gather1(0, 4)
         gather1(1, 4)
 
         windows = [held.tile([P, T], F32, name=name, align_bytes=64) for name in ("pair10", "pair11")]
@@ -247,12 +245,13 @@ def tile_moe_shr_lin_relu2_kernel(tc, xT, w_words, w_scales, b, gate, offs, out)
 
         both = [(0, 1)]
         unit(*spans[0], 0, both, ())
+        late = held.tile([P, 4 * Q], U32, name=f"sq_y{7 * C}_0", align_bytes=64)
+        weave(late[:, 2 * Q : 4 * Q], stage1[3])
+        weave(late[:, 0 : 2 * Q], stage1[4])
+        quantize(1, 0, 2 * Q, late[:])
         unit(*spans[1], 4, both, ())
-        for i, name in ((3, f"sq_s{7 * C}_0"), (4, f"sq_y{6 * C}_0")):
-            weave1(i, name)
-            quantize1(i)
         unit(*spans[2], 0, [(0,), (1,)], ())
-        unit(Q, Q, 0, both, (1,))
+        unit(Q, Q, 0, both, ())
         unit(0, Q, 0, both, (0, 1))
         for h in range(2):
             nc.sync.dma_start(out[P * h : P * h + P, :], windows[h][:])

@@ -34,10 +34,6 @@ def tile_moe_shr_lin_relu2_kernel(tc, xT, w_words, w_scales, b, gate, offs, out)
 
         offsets = held.tile([P, T // 16], U16, name="offsets")
 
-        dummy = held.tile([P, 1], F32, name="dummy")
-        nc.vector.memset(dummy[:], 0.0)
-        nc.scalar.activation(dummy[:], dummy[:], RELU)
-
         firsts = [T - Q * (q + 1) for q in range(NQ)]
 
         w_at = {}
@@ -74,7 +70,7 @@ def tile_moe_shr_lin_relu2_kernel(tc, xT, w_words, w_scales, b, gate, offs, out)
                     s_view[first : first + count, :, 4 * quad : 4 * quad + 4, :].rearrange("e a q n -> q (e a) n"),
                 )
 
-        bias = held.tile([P, 2, E + 1], F32, name="bias")
+        bias = held.tile([P, 2, 16], F32, name="bias")
         gates = [held.tile([P, 512], F32, name=f"gates{i}") for i in range(2)]
 
         load_x(0, 0)
@@ -84,7 +80,7 @@ def tile_moe_shr_lin_relu2_kernel(tc, xT, w_words, w_scales, b, gate, offs, out)
         load_x(1, 1)
         load_scales(6, 3)
         load_w(6, 3)
-        nc.sync.dma_start(bias[:], b.rearrange("(h p) e -> p h e", p=P))
+        nc.sync.dma_start(bias[:, :, 0 : E + 1], b.rearrange("(h p) e -> p h e", p=P))
         nc.sync.dma_start(gates[1][:], gate[0:P, 512:T])
         load_w(4, 2)
         load_scales(0, 6)
@@ -137,7 +133,7 @@ def tile_moe_shr_lin_relu2_kernel(tc, xT, w_words, w_scales, b, gate, offs, out)
         stage1 = {}
 
         def gather1(u, i):
-            gather(1, u, woven1[i][:, :, u] if i < 2 else stage1[i][:, u, :], *spans[i])
+            gather(1, u, stage1[i][:, u, :] if i in stage1 else woven1[i][:, :, u], *spans[i])
 
         def weave1(i, name):
             woven1[i] = held.tile([P, Q, 2], U32, name=name, align_bytes=64)
@@ -148,9 +144,11 @@ def tile_moe_shr_lin_relu2_kernel(tc, xT, w_words, w_scales, b, gate, offs, out)
         for i in range(2):
             woven1[i] = held.tile([P, C, 2], U32, name=f"woven1_{i}", align_bytes=64)
             gather1(0, i)
-        for i in (2, 3, 4):
+        for i in (2, 3):
             stage1[i] = held.tile([P, 2, Q], U32, name=f"stage1_{i}", align_bytes=64)[:]
             gather1(0, i)
+        woven1[4] = held.tile([P, Q, 2], U32, name="woven1_4", align_bytes=64)
+        gather1(0, 4)
         weave0([1], "raw101")
         cast(1, 1, [("S", 0, 256), ("G", 256, 512), ("S", 512, 832), ("G", 832, 1024)])
         weave0([2, 3], "raw110")
@@ -180,6 +178,7 @@ def tile_moe_shr_lin_relu2_kernel(tc, xT, w_words, w_scales, b, gate, offs, out)
         quantize1(2)
         gather1(1, 3)
         gather1(1, 4)
+        quantize1(4)
 
         windows = [held.tile([P, T], F32, name=name, align_bytes=64) for name in ("pair10", "pair11")]
 
@@ -245,13 +244,11 @@ def tile_moe_shr_lin_relu2_kernel(tc, xT, w_words, w_scales, b, gate, offs, out)
 
         both = [(0, 1)]
         unit(*spans[0], 0, both, ())
-        late = held.tile([P, 4 * Q], U32, name=f"sq_y{7 * C}_0", align_bytes=64)
-        weave(late[:, 2 * Q : 4 * Q], stage1[3])
-        weave(late[:, 0 : 2 * Q], stage1[4])
-        quantize(1, 0, 2 * Q, late[:])
+        weave1(3, f"sq_y{7 * C}_0")
+        quantize1(3)
         unit(*spans[1], 4, both, ())
         unit(*spans[2], 0, [(0,), (1,)], ())
-        unit(Q, Q, 0, both, ())
+        unit(Q, Q, 0, [(0,), (1,)], ())
         unit(0, Q, 0, both, (0, 1))
         for h in range(2):
             nc.sync.dma_start(out[P * h : P * h + P, :], windows[h][:])

@@ -144,11 +144,9 @@ def tile_moe_shr_lin_relu2_kernel(tc, xT, w_words, w_scales, b, gate, offs, out)
         for i in range(2):
             woven1[i] = held.tile([P, C, 2], U32, name=f"woven1_{i}", align_bytes=64)
             gather1(0, i)
-        for i in (2, 3):
+        for i in (2, 3, 4):
             stage1[i] = held.tile([P, 2, Q], U32, name=f"stage1_{i}", align_bytes=64)[:]
             gather1(0, i)
-        woven1[4] = held.tile([P, Q, 2], U32, name="woven1_4", align_bytes=64)
-        gather1(0, 4)
         weave0([1], "raw101")
         cast(1, 1, [("S", 0, 256), ("G", 256, 512), ("S", 512, 832), ("G", 832, 1024)])
         weave0([2, 3], "raw110")
@@ -168,17 +166,16 @@ def tile_moe_shr_lin_relu2_kernel(tc, xT, w_words, w_scales, b, gate, offs, out)
         gather1(1, 0)
         quantize(0, firsts[0], Q, woven0[0])
         quantize1(0)
-        gather1(1, 2)
-        weave1(2, "woven1_2")
+        for i in (2, 3, 4):
+            gather1(1, i)
+            weave1(i, f"woven1_{i}")
         gather1(1, 1)
         quantize(0, firsts[1], Q, woven0[1])
         quantize1(1)
         quantize(0, firsts[2], Q, woven0[2])
         quantize(0, firsts[3], Q, woven0[3])
-        quantize1(2)
-        gather1(1, 3)
-        gather1(1, 4)
-        quantize1(4)
+        for i in (2, 3, 4):
+            quantize1(i)
 
         windows = [held.tile([P, T], F32, name=name, align_bytes=64) for name in ("pair10", "pair11")]
 
@@ -196,7 +193,7 @@ def tile_moe_shr_lin_relu2_kernel(tc, xT, w_words, w_scales, b, gate, offs, out)
                     stop=(a == A - 1),
                 )
 
-        def unit(first, count, banks, groups, fused):
+        def unit(first, count, banks, groups, fused, engine=nc.gpsimd):
             blocks = range(first // C, (first + count) // C)
             y = [psum.tile([P, count], F32, name=f"bank{banks + h}") for h in range(2)]
             s = [psum.tile([P, count], F32, name=f"bank{banks + 2 + h}") for h in range(2)]
@@ -218,7 +215,7 @@ def tile_moe_shr_lin_relu2_kernel(tc, xT, w_words, w_scales, b, gate, offs, out)
                     for j, e in enumerate(blocks):
                         nc.scalar.activation(r_y[:, i, C * j : C * j + C], y[h][:, C * j : C * j + C], RELU, bias=bias[:, h, e : e + 1])
                 nc.scalar.activation(sq_y[:], r_y[:], SQUARE)
-                nc.gpsimd.tensor_tensor(t[:], sq_y[:], weights.unsqueeze(1).to_broadcast([P, n, count]), MULT)
+                engine.tensor_tensor(t[:], sq_y[:], weights.unsqueeze(1).to_broadcast([P, n, count]), MULT)
                 if count == C:
                     r_s = ring.tile([P, n, count], F32, name="r")
                     sq_s = held.tile([P, n, count], F32, name=f"sq_s{tag}", align_bytes=64)
@@ -226,7 +223,7 @@ def tile_moe_shr_lin_relu2_kernel(tc, xT, w_words, w_scales, b, gate, offs, out)
                     for i, h in enumerate(group):
                         nc.scalar.activation(r_s[:, i, :], s[h][:], RELU, bias=bias[:, h, E : E + 1])
                     nc.scalar.activation(sq_s[:], r_s[:], SQUARE)
-                    nc.gpsimd.tensor_tensor(o[:], t[:], sq_s[:], ADD)
+                    engine.tensor_tensor(o[:], t[:], sq_s[:], ADD)
                     for i, h in enumerate(group):
                         nc.vector.tensor_copy(places[h], o[:, i, :])
                     continue
@@ -243,9 +240,7 @@ def tile_moe_shr_lin_relu2_kernel(tc, xT, w_words, w_scales, b, gate, offs, out)
                         nc.vector.tensor_copy(places[h], o[:])
 
         both = [(0, 1)]
-        unit(*spans[0], 0, both, ())
-        weave1(3, f"sq_y{7 * C}_0")
-        quantize1(3)
+        unit(*spans[0], 0, both, (), nc.vector)
         unit(*spans[1], 4, both, ())
         unit(*spans[2], 0, [(0,), (1,)], ())
         unit(Q, Q, 0, [(0,), (1,)], ())

@@ -54,6 +54,15 @@ def tile_moe_shr_lin_relu2_kernel(tc, xT, w_words, w_scales, b, gate, offs, out)
                 nc.sync.dma_start(raw[:], x_view[a, u][:, :, 512 * s : 512 * s + 512])
                 raws[a, u, s] = raw
 
+        x_rows = xT.rearrange("(a p u e) n -> a u p (e n)", p=P, u=2, e=2)
+
+        def load_long(a, u):
+            raw = held.tile([P, 2 * T], F32, name=f"raw{a}{u}1", align_bytes=64)
+            nc.sync.dma_start(raw[:, 0 : T + 512], x_rows[a, u][:, 0 : T + 512])
+            nc.sync.dma_start(raw[:, T + 512 : 2 * T], x_rows[a, u][:, T + 512 : 2 * T])
+            for s in range(2):
+                raws[a, u, s] = raw[:].rearrange("p (e n) -> p e n", e=2)[:, :, 512 * s : 512 * s + 512]
+
         w_view = w_words.bitcast(I32)
         s_view = w_scales.bitcast(I32)
 
@@ -73,10 +82,10 @@ def tile_moe_shr_lin_relu2_kernel(tc, xT, w_words, w_scales, b, gate, offs, out)
         bias = held.tile([P, 2, 16], F32, name="bias")
         gates = [held.tile([P, 512], F32, name=f"gates{i}") for i in range(2)]
 
-        load_x(0, 0)
+        load_long(0, 0)
         nc.sync.dma_start(offsets[:], offs)
-        load_x(0, 1)
-        load_x(1, 0)
+        load_long(0, 1)
+        load_long(1, 0)
         load_x(1, 1)
         load_scales(6, 3)
         load_w(6, 3)
@@ -110,10 +119,10 @@ def tile_moe_shr_lin_relu2_kernel(tc, xT, w_words, w_scales, b, gate, offs, out)
         codes = {}
         scales = {}
 
-        shared = [("S", 0, 128), ("G", 128, 512), ("S", 512, 832), ("G", 832, 1024)]
+        shared = [("S", 0, 320), ("G", 320, 512), ("S", 512, 832), ("G", 832, 1024)]
 
         stage0 = held.tile([P, 2, T], U32, name="stage0", align_bytes=64)
-        cast(0, 0, [("S", 0, 256), ("V", 256, 512), ("S", 512, 672), ("V", 672, 1024)])
+        cast(0, 0, [("S", 0, 160), ("V", 160, 512), ("S", 512, 672), ("V", 672, 1024)])
         for first in (512, 0):
             gather(0, 0, stage0[:, 0, first : first + 512], first, 512)
         cast(0, 1, shared)
@@ -139,7 +148,7 @@ def tile_moe_shr_lin_relu2_kernel(tc, xT, w_words, w_scales, b, gate, offs, out)
             woven1[i] = held.tile([P, Q, 2], U32, name=name, align_bytes=64)
             weave(woven1[i][:].rearrange("p n u -> p (n u)"), stage1[i])
 
-        cast(1, 0, shared)
+        cast(1, 0, [("S", 0, 160), ("G", 160, 512), ("S", 512, 832), ("G", 832, 1024)])
         weave0([0], "woven00")
         for i in range(2):
             woven1[i] = held.tile([P, C, 2], U32, name=f"woven1_{i}", align_bytes=64)

@@ -16,8 +16,10 @@ FP4X4 = mybir.dt.float4_e2m1fn_x4
 
 ADD = mybir.AluOpType.add
 MULT = mybir.AluOpType.mult
+MAX = mybir.AluOpType.max
 RELU = mybir.ActivationFunctionType.Relu
 SQUARE = mybir.ActivationFunctionType.Square
+COPY = mybir.ActivationFunctionType.Copy
 
 P = 128
 A = K // 512
@@ -39,7 +41,7 @@ def tile_moe_shr_lin_relu2_kernel(tc, xT, w_words, w_scales, b, gate, offs, out)
         w_at = {}
         s_at = {}
         planes = {}
-        for first, count in ((6, 3), (0, 6)):
+        for first, count in ((4, 5), (0, 4)):
             planes[first] = held.tile([P, count * A, N], U8, name=f"planes{first}", align_bytes=64)
             nc.gpsimd.memset(planes[first][:].bitcast(I32), 0)
             for i in range(count):
@@ -87,12 +89,12 @@ def tile_moe_shr_lin_relu2_kernel(tc, xT, w_words, w_scales, b, gate, offs, out)
         load_long(0, 1)
         load_long(1, 0)
         load_x(1, 1)
-        load_scales(6, 3)
+        load_scales(4, 5)
         load_w(6, 3)
+        load_w(4, 2)
         nc.sync.dma_start(bias[:, :, 0 : E + 1], b.rearrange("(h p) e -> p h e", p=P))
         nc.sync.dma_start(gates[1][:], gate[0:P, 512:T])
-        load_w(4, 2)
-        load_scales(0, 6)
+        load_scales(0, 4)
         load_w(0, 4)
         nc.sync.dma_start(gates[0][:], gate[0:P, 0:512])
 
@@ -165,9 +167,11 @@ def tile_moe_shr_lin_relu2_kernel(tc, xT, w_words, w_scales, b, gate, offs, out)
             code = codes0[:, first : first + count] if a == 0 else held.tile([P, count], U32, name=f"codes1_{first}", align_bytes=64)[:]
             scale = held.tile([P, count], U8, name=f"scales{a}_{first}", align_bytes=64)
             nc.vector.quantize_mx(out=code.bitcast(FP8X4), scales=scale[:], in_=words.bitcast(BF16))
+            codes[a, first, count] = code
+            scales[a, first, count] = scale[:]
             for at in range(0, count, C):
-                codes[a, (first + at) // C] = code[:, at : at + C]
-                scales[a, (first + at) // C] = scale[:, at : at + C]
+                codes[a, first + at, C] = code[:, at : at + C]
+                scales[a, first + at, C] = scale[:, at : at + C]
 
         def quantize1(i):
             quantize(1, *spans[i], woven1[i][:].rearrange("p n u -> p (n u)"))
@@ -175,84 +179,117 @@ def tile_moe_shr_lin_relu2_kernel(tc, xT, w_words, w_scales, b, gate, offs, out)
         gather1(1, 0)
         quantize(0, firsts[0], Q, woven0[0])
         quantize1(0)
+        quantize(0, firsts[1], Q, woven0[1])
         for i in (2, 3, 4):
             gather1(1, i)
             weave1(i, f"woven1_{i}")
         gather1(1, 1)
-        quantize(0, firsts[1], Q, woven0[1])
         quantize1(1)
-        quantize(0, firsts[2], Q, woven0[2])
-        quantize(0, firsts[3], Q, woven0[3])
-        for i in (2, 3, 4):
+        quantize1(2)
+        for i in (3, 4):
+            quantize(0, firsts[i - 1], Q, woven0[i - 1])
             quantize1(i)
 
-        windows = [held.tile([P, T], F32, name=name, align_bytes=64) for name in ("pair10", "pair11")]
+        banks = {}
 
-        def product(out_ap, e, h, block):
-            words, at = w_at[e]
-            plane, at_s = s_at[e]
-            for a in range(A):
+        def passes(a, first, count, halves):
+            if a == 0:
+                banks[first, halves] = psum.tile([P, 512], F32, name=f"bank{first}_{halves[0]}")
+            jobs = [(first // C + j, h, first + C * j, C) for h in halves for j in range(count // C)]
+            jobs = jobs + [(E, h, first, count) for h in halves]
+            col = 0
+            for i, (e, h, start, width) in enumerate(jobs):
+                words, at = w_at[e]
+                plane, at_s = s_at[e]
                 nc.tensor.matmul_mx(
-                    out=out_ap,
+                    out=banks[first, halves][:, col : col + width],
                     lhsT=words[:, at + a, N * h : N * h + N].bitcast(FP4X4),
                     lhsT_scale=plane[:, at_s + a, P * h : P * h + P],
-                    rhs=codes[a, block].bitcast(FP8X4),
-                    rhs_scale=scales[a, block],
-                    start=(a == 0),
-                    stop=(a == A - 1),
+                    rhs=codes[a, start, width].bitcast(FP8X4),
+                    rhs_scale=scales[a, start, width],
+                    start=(a == 0 and i == 0),
+                    stop=(a == A - 1 and i == len(jobs) - 1),
                 )
+                col = col + width
 
-        def unit(first, count, banks, groups, fused, engine=nc.gpsimd):
-            blocks = range(first // C, (first + count) // C)
-            y = [psum.tile([P, count], F32, name=f"bank{banks + h}") for h in range(2)]
-            s = [psum.tile([P, count], F32, name=f"bank{banks + 2 + h}") for h in range(2)]
-            weights = gates[first // 512][:, first % 512 : first % 512 + count]
+        passes(0, 7 * C, C, (0, 1))
+        passes(1, 7 * C, C, (0, 1))
+        passes(0, 6 * C, C, (0, 1))
+        for h in (1, 0):
+            passes(0, 2 * Q, Q, (h,))
+        passes(1, 6 * C, C, (0, 1))
+        for h in (1, 0):
+            passes(1, 2 * Q, Q, (h,))
+        for first in (Q, 0):
+            for h in (1, 0):
+                for a in range(A):
+                    passes(a, first, Q, (h,))
+
+        sums = {}
+
+        def weights(first, count):
+            return gates[first // 512][:, first % 512 : first % 512 + count]
+
+        def single(first, combine, name):
+            e = first // C
+            bank = banks[first, (0, 1)][:].rearrange("p (j c) -> p j c", c=C)
+            r = held.tile([P, 4, C], F32, name=f"r{first}")
+            sq = held.tile([P, 4, C], F32, name=f"sq{first}", align_bytes=64)
+            t = held.tile([P, 2, C], F32, name=name)
+            o = held.tile([P, 2, C], F32, name=f"o{first}")
+            for j in range(4):
+                column = (e, E)[j // 2]
+                nc.scalar.activation(r[:, j, :], bank[:, j, :], RELU, bias=bias[:, j % 2, column : column + 1])
+            nc.scalar.activation(sq[:], r[:], SQUARE)
+            combine.tensor_tensor(t[:], sq[:, 0:2, :], weights(first, C).unsqueeze(1).to_broadcast([P, 2, C]), MULT)
+            combine.tensor_tensor(o[:], t[:], sq[:, 2:4, :], ADD)
+            for h in range(2):
+                sums[first, h] = o[:, h, :]
+
+        def half_on_scalar(first, name):
+            bank = banks[first, (1,)]
+            r = held.tile([P, 2 * Q], F32, name=name, align_bytes=64)
+            sq = held.tile([P, 2 * Q], F32, name=f"sq{first}_1")
+            t = held.tile([P, Q], F32, name="t")
+            o = held.tile([P, Q], F32, name=f"o{first}_1")
+            for column, at, width in ((first // C, 0, C), (first // C + 1, C, C), (E, Q, Q)):
+                nc.scalar.activation(r[:, at : at + width], bank[:, at : at + width], RELU, bias=bias[:, 1, column : column + 1])
+            nc.scalar.activation(sq[:], r[:], SQUARE)
+            nc.gpsimd.tensor_tensor(t[:], sq[:, 0:Q], weights(first, Q), MULT)
+            return t, sq, o
+
+        def half_on_vector(first, name):
+            bank = banks[first, (0,)]
+            r_y = held.tile([P, Q], F32, name=f"r_y{first}")
+            r_s = held.tile([P, Q], F32, name=name, align_bytes=64)
+            u = held.tile([P, Q], F32, name=f"u{first}")
+            sq_s = held.tile([P, Q], F32, name=f"sq_s{first}")
+            t = held.tile([P, Q], F32, name=f"t{first}_0")
+            experts = [(first // C + j, slice(C * j, C * j + C)) for j in range(2)]
+            shared_bias = bias[:, 0, E : E + 1]
+            nc.vector.tensor_scalar(r_s[:], bank[:, Q : 2 * Q], shared_bias, 0.0, ADD, MAX)
+            for e, cols in experts:
+                nc.vector.tensor_scalar(r_y[:, cols], bank[:, cols], bias[:, 0, e : e + 1], 0.0, ADD, MAX)
+            for e, cols in experts:
+                nc.vector.scalar_tensor_tensor(u[:, cols], bank[:, cols], bias[:, 0, e : e + 1], weights(e * C, C), ADD, MULT)
+            nc.vector.scalar_tensor_tensor(sq_s[:], bank[:, Q : 2 * Q], shared_bias, r_s[:], ADD, MULT)
+            nc.gpsimd.tensor_tensor(t[:], u[:], r_y[:], MULT)
+            sums[first, 0] = (t[:], sq_s[:])
+
+        single(7 * C, nc.vector, "t_first")
+        single(6 * C, nc.gpsimd, "t")
+        for first in (2 * Q, Q, 0):
+            t, sq, o = half_on_scalar(first, "window1" if first == 0 else f"r{first}_1")
+            half_on_vector(first, "window0" if first == 0 else f"r_s{first}")
+            nc.gpsimd.tensor_tensor(o[:], t[:], sq[:, Q : 2 * Q], ADD)
+            sums[first, 1] = o[:]
+        windows = [held.tile([P, T], F32, name=f"window{h}", align_bytes=64) for h in range(2)]
+        for first, count in spans:
             places = [windows[h][:].indirect(offsets[:, first // 16 : (first + count) // 16]) for h in range(2)]
-            for group in groups:
-                n = len(group)
-                tag = f"{first}_{group[0]}"
-                for h in group:
-                    for j, e in enumerate(blocks):
-                        product(y[h][:, C * j : C * j + C], e, h, e)
-                for h in group:
-                    for j, e in enumerate(blocks):
-                        product(s[h][:, C * j : C * j + C], E, h, e)
-                r_y = ring.tile([P, n, count], F32, name="r")
-                sq_y = held.tile([P, n, count], F32, name=f"sq_y{tag}", align_bytes=64)
-                t = held.tile([P, n, count], F32, name=f"t{tag}")
-                for i, h in enumerate(group):
-                    for j, e in enumerate(blocks):
-                        nc.scalar.activation(r_y[:, i, C * j : C * j + C], y[h][:, C * j : C * j + C], RELU, bias=bias[:, h, e : e + 1])
-                nc.scalar.activation(sq_y[:], r_y[:], SQUARE)
-                engine.tensor_tensor(t[:], sq_y[:], weights.unsqueeze(1).to_broadcast([P, n, count]), MULT)
-                if count == C:
-                    r_s = ring.tile([P, n, count], F32, name="r")
-                    sq_s = held.tile([P, n, count], F32, name=f"sq_s{tag}", align_bytes=64)
-                    o = held.tile([P, n, count], F32, name=f"o{tag}")
-                    for i, h in enumerate(group):
-                        nc.scalar.activation(r_s[:, i, :], s[h][:], RELU, bias=bias[:, h, E : E + 1])
-                    nc.scalar.activation(sq_s[:], r_s[:], SQUARE)
-                    engine.tensor_tensor(o[:], t[:], sq_s[:], ADD)
-                    for i, h in enumerate(group):
-                        nc.vector.tensor_copy(places[h], o[:, i, :])
-                    continue
-                for i, h in enumerate(group):
-                    r_s = ring.tile([P, count], F32, name="r")
-                    sq_s = held.tile([P, count], F32, name=f"sq_s{first}_{h}")
-                    nc.scalar.activation(r_s[:], s[h][:], RELU, bias=bias[:, h, E : E + 1])
-                    nc.scalar.activation(sq_s[:], r_s[:], SQUARE)
-                    if h in fused:
-                        nc.vector.tensor_tensor(places[h], t[:, i, :], sq_s[:], ADD)
-                    else:
-                        o = held.tile([P, count], F32, name=f"o{first}_{h}")
-                        nc.gpsimd.tensor_tensor(o[:], t[:, i, :], sq_s[:], ADD)
-                        nc.vector.tensor_copy(places[h], o[:])
-
-        both = [(0, 1)]
-        unit(*spans[0], 0, both, (), nc.vector)
-        unit(*spans[1], 4, both, ())
-        unit(*spans[2], 0, [(0,), (1,)], ())
-        unit(Q, Q, 0, [(0,), (1,)], ())
-        unit(0, Q, 0, both, (0, 1))
+            if count == Q:
+                nc.vector.tensor_tensor(places[0], *sums[first, 0], ADD)
+            else:
+                nc.vector.tensor_copy(places[0], sums[first, 0])
+            nc.scalar.activation(places[1], sums[first, 1], COPY)
         for h in range(2):
             nc.sync.dma_start(out[P * h : P * h + P, :], windows[h][:])

@@ -148,7 +148,10 @@ def tile_moe_shr_lin_relu2_kernel(tc, xT, w_words, w_scales, b, gate, offs, out)
 
         def weave1(i, name):
             woven1[i] = held.tile([P, Q, 2], U32, name=name, align_bytes=64)
-            weave(woven1[i][:].rearrange("p n u -> p (n u)"), stage1[i])
+            if i == 4:
+                nc.vector.tensor_copy(woven1[i][:].bitcast(I32), stage1[i].bitcast(I32).rearrange("p u n -> p n u"))
+            else:
+                weave(woven1[i][:].rearrange("p n u -> p (n u)"), stage1[i])
 
         cast(1, 0, [("S", 0, 160), ("G", 160, 512), ("S", 512, 832), ("G", 832, 1024)])
         weave0([0], "woven00")
@@ -165,7 +168,7 @@ def tile_moe_shr_lin_relu2_kernel(tc, xT, w_words, w_scales, b, gate, offs, out)
 
         def quantize(a, first, count, words):
             code = codes0[:, first : first + count] if a == 0 else held.tile([P, count], U32, name=f"codes1_{first}", align_bytes=64)[:]
-            scale = held.tile([P, count], U8, name=f"scales{a}_{first}", align_bytes=64)
+            scale = held.tile([P, count], U8, name="woven1_3" if (a, first) == (1, 0) else f"scales{a}_{first}", align_bytes=64)
             nc.vector.quantize_mx(out=code.bitcast(FP8X4), scales=scale[:], in_=words.bitcast(BF16))
             codes[a, first, count] = code
             scales[a, first, count] = scale[:]
@@ -190,106 +193,125 @@ def tile_moe_shr_lin_relu2_kernel(tc, xT, w_words, w_scales, b, gate, offs, out)
             quantize(0, firsts[i - 1], Q, woven0[i - 1])
             quantize1(i)
 
+        first_expert, second_expert, unit_b, unit_c, unit_d = spans
+
         banks = {}
 
-        def passes(a, first, count, halves):
+        def passes(a, name, jobs):
             if a == 0:
-                banks[first, halves] = psum.tile([P, 512], F32, name=f"bank{first}_{halves[0]}")
-            jobs = [(first // C + j, h, first + C * j, C) for h in halves for j in range(count // C)]
-            jobs = jobs + [(E, h, first, count) for h in halves]
+                banks[name] = psum.tile([P, 2, Q], F32, name=name)
+            flat = banks[name][:].rearrange("p j c -> p (j c)")
             col = 0
-            for i, (e, h, start, width) in enumerate(jobs):
+            for i, (e, h, first, count) in enumerate(jobs):
                 words, at = w_at[e]
                 plane, at_s = s_at[e]
                 nc.tensor.matmul_mx(
-                    out=banks[first, halves][:, col : col + width],
+                    out=flat[:, col : col + count],
                     lhsT=words[:, at + a, N * h : N * h + N].bitcast(FP4X4),
                     lhsT_scale=plane[:, at_s + a, P * h : P * h + P],
-                    rhs=codes[a, start, width].bitcast(FP8X4),
-                    rhs_scale=scales[a, start, width],
+                    rhs=codes[a, first, count].bitcast(FP8X4),
+                    rhs_scale=scales[a, first, count],
                     start=(a == 0 and i == 0),
                     stop=(a == A - 1 and i == len(jobs) - 1),
                 )
-                col = col + width
+                col = col + count
 
-        passes(0, 7 * C, C, (0, 1))
-        passes(1, 7 * C, C, (0, 1))
-        passes(0, 6 * C, C, (0, 1))
-        for h in (1, 0):
-            passes(0, 2 * Q, Q, (h,))
-        passes(1, 6 * C, C, (0, 1))
-        for h in (1, 0):
-            passes(1, 2 * Q, Q, (h,))
-        for first in (Q, 0):
-            for h in (1, 0):
-                for a in range(A):
-                    passes(a, first, Q, (h,))
+        def routed(first, h):
+            return [(first // C + j, h, first + C * j, C) for j in range(2)]
 
-        sums = {}
+        jobs = {}
+        for name, span in (("first", first_expert), ("second", second_expert)):
+            jobs[name] = [(e, h, *span) for e in (span[0] // C, E) for h in range(2)]
+        for name, (first, count) in (("b", unit_b), ("c", unit_c), ("d", unit_d)):
+            jobs["y" + name] = routed(first, 0) + routed(first, 1)
+            jobs["s" + name] = [(E, h, first, count) for h in range(2)]
+
+        def multiply(a, names):
+            for name in names:
+                passes(a, name, jobs[name])
 
         def weights(first, count):
             return gates[first // 512][:, first % 512 : first % 512 + count]
 
-        def single(first, combine, name):
-            e = first // C
-            bank = banks[first, (0, 1)][:].rearrange("p (j c) -> p j c", c=C)
-            r = held.tile([P, 4, C], F32, name=f"r{first}")
-            sq = held.tile([P, 4, C], F32, name=f"sq{first}", align_bytes=64)
-            t = held.tile([P, 2, C], F32, name=name)
-            o = held.tile([P, 2, C], F32, name=f"o{first}")
-            for j in range(4):
-                column = (e, E)[j // 2]
-                nc.scalar.activation(r[:, j, :], bank[:, j, :], RELU, bias=bias[:, j % 2, column : column + 1])
-            nc.scalar.activation(sq[:], r[:], SQUARE)
-            combine.tensor_tensor(t[:], sq[:, 0:2, :], weights(first, C).unsqueeze(1).to_broadcast([P, 2, C]), MULT)
-            combine.tensor_tensor(o[:], t[:], sq[:, 2:4, :], ADD)
-            for h in range(2):
-                sums[first, h] = o[:, h, :]
+        def squares_on_scalar(name, r_name):
+            flat = banks[name][:].rearrange("p j c -> p (j c)")
+            r = held.tile([P, 2 * Q], F32, name=r_name, align_bytes=64)
+            sq = held.tile([P, 2, Q], F32, name=f"sq_{name}")
+            col = 0
+            for e, h, first, count in jobs[name]:
+                nc.scalar.activation(r[:, col : col + count], flat[:, col : col + count], RELU, bias=bias[:, h, e : e + 1])
+                col = col + count
+            nc.scalar.activation(sq[:].rearrange("p j c -> p (j c)"), r[:], SQUARE)
+            return sq
 
-        def half_on_scalar(first, name):
-            bank = banks[first, (1,)]
-            r = held.tile([P, 2 * Q], F32, name=name, align_bytes=64)
-            sq = held.tile([P, 2 * Q], F32, name=f"sq{first}_1")
-            t = held.tile([P, Q], F32, name="t")
-            o = held.tile([P, Q], F32, name=f"o{first}_1")
-            for column, at, width in ((first // C, 0, C), (first // C + 1, C, C), (E, Q, Q)):
-                nc.scalar.activation(r[:, at : at + width], bank[:, at : at + width], RELU, bias=bias[:, 1, column : column + 1])
-            nc.scalar.activation(sq[:], r[:], SQUARE)
-            nc.gpsimd.tensor_tensor(t[:], sq[:, 0:Q], weights(first, Q), MULT)
-            return t, sq, o
+        def squares_on_vector(sums, outs, r_names):
+            r = [held.tile([P, sums[h].shape[1]], F32, name=r_names[h], align_bytes=64) for h in range(2)]
+            for h in (1, 0):
+                nc.vector.tensor_scalar(r[h][:], sums[h], bias[:, h, E : E + 1], 0.0, ADD, MAX)
+            for h in (1, 0):
+                nc.vector.scalar_tensor_tensor(outs[h], sums[h], bias[:, h, E : E + 1], r[h][:], ADD, MULT)
 
-        def half_on_vector(first, name):
-            bank = banks[first, (0,)]
-            r_y = held.tile([P, Q], F32, name=f"r_y{first}")
-            r_s = held.tile([P, Q], F32, name=name, align_bytes=64)
-            u = held.tile([P, Q], F32, name=f"u{first}")
-            sq_s = held.tile([P, Q], F32, name=f"sq_s{first}")
-            t = held.tile([P, Q], F32, name=f"t{first}_0")
-            experts = [(first // C + j, slice(C * j, C * j + C)) for j in range(2)]
-            shared_bias = bias[:, 0, E : E + 1]
-            nc.vector.tensor_scalar(r_s[:], bank[:, Q : 2 * Q], shared_bias, 0.0, ADD, MAX)
-            for e, cols in experts:
-                nc.vector.tensor_scalar(r_y[:, cols], bank[:, cols], bias[:, 0, e : e + 1], 0.0, ADD, MAX)
-            for e, cols in experts:
-                nc.vector.scalar_tensor_tensor(u[:, cols], bank[:, cols], bias[:, 0, e : e + 1], weights(e * C, C), ADD, MULT)
-            nc.vector.scalar_tensor_tensor(sq_s[:], bank[:, Q : 2 * Q], shared_bias, r_s[:], ADD, MULT)
-            nc.gpsimd.tensor_tensor(t[:], u[:], r_y[:], MULT)
-            sums[first, 0] = (t[:], sq_s[:])
+        sums = held.tile([P, 2, T], F32, name="sums", align_bytes=64)
 
-        single(7 * C, nc.vector, "t_first")
-        single(6 * C, nc.gpsimd, "t")
-        for first in (2 * Q, Q, 0):
-            t, sq, o = half_on_scalar(first, "window1" if first == 0 else f"r{first}_1")
-            half_on_vector(first, "window0" if first == 0 else f"r_s{first}")
-            nc.gpsimd.tensor_tensor(o[:], t[:], sq[:, Q : 2 * Q], ADD)
-            sums[first, 1] = o[:]
-        windows = [held.tile([P, T], F32, name=f"window{h}", align_bytes=64) for h in range(2)]
-        for first, count in spans:
-            places = [windows[h][:].indirect(offsets[:, first // 16 : (first + count) // 16]) for h in range(2)]
-            if count == Q:
-                nc.vector.tensor_tensor(places[0], *sums[first, 0], ADD)
+        def gated(engine, sq, span, name):
+            t = held.tile([P, 2, span[1]], F32, name=name, align_bytes=64)
+            engine.tensor_tensor(t[:], sq, weights(*span).unsqueeze(1).to_broadcast([P, 2, span[1]]), MULT)
+            return t
+
+        def total(engine, span, t, sq_s):
+            engine.tensor_tensor(sums[:, :, span[0] : span[0] + span[1]], t[:], sq_s, ADD)
+
+        multiply(0, ("first",))
+        multiply(1, ("first",))
+        multiply(0, ("second", "yb", "sb"))
+        multiply(1, ("second", "yb", "sb"))
+        for name in ("yc", "sc", "yd", "sd"):
+            for a in range(A):
+                multiply(a, (name,))
+
+        def single(name, span, engine, t_name):
+            bank = banks[name][:].rearrange("p j (h c) -> p j h c", h=2)
+            sq = held.tile([P, 2, 2, C], F32, name=f"sq_{name}")
+            for j in range(2):
+                r = ring.tile([P, 2, C], F32, name="r")
+                e = jobs[name][2 * j][0]
+                for h in range(2):
+                    nc.scalar.activation(r[:, h, :], bank[:, j, h, :], RELU, bias=bias[:, h, e : e + 1])
+                nc.scalar.activation(sq[:, j], r[:], SQUARE)
+            total(engine, span, gated(engine, sq[:, 0], span, t_name), sq[:, 1])
+
+        single("first", first_expert, nc.vector, "t")
+        single("second", second_expert, nc.gpsimd, "woven1_4")
+        windows = {0: held.tile([P, T], F32, name="pair10", align_bytes=64)}
+
+        def place_of(span, h):
+            first, count = span
+            return windows[h][:].indirect(offsets[:, first // 16 : (first + count) // 16])
+
+        def scatter(span, h):
+            source = sums[:, h, span[0] : span[0] + span[1]]
+            if h == 0:
+                nc.vector.tensor_copy(place_of(span, 0), source)
             else:
-                nc.vector.tensor_copy(places[0], sums[first, 0])
-            nc.scalar.activation(places[1], sums[first, 1], COPY)
+                nc.scalar.activation(place_of(span, 1), source, COPY)
+
+        unit_a = (3 * Q, Q)
+        for name, span in (("b", unit_b), ("c", unit_c), ("d", unit_d)):
+            sq_s = held.tile([P, 2, Q], F32, name=f"sq_s{name}")
+            squares_on_vector([banks["s" + name][:, h, :] for h in range(2)], [sq_s[:, h, :] for h in range(2)], (f"r_s{name}0", f"r_s{name}1"))
+            if name == "c":
+                scatter(unit_a, 0)
+            if name == "d":
+                windows[1] = held.tile([P, T], F32, name="window1", align_bytes=64)
+                scatter(unit_a, 1)
+            t = gated(nc.gpsimd, squares_on_scalar("y" + name, "window1" if name == "c" else f"r_y{name}")[:], span, "t")
+            if name != "d":
+                total(nc.gpsimd, span, t, sq_s[:])
+        nc.gpsimd.tensor_tensor(sums[:, 1, 0:Q], t[:, 1, :], sq_s[:, 1, :], ADD)
+        for span in (unit_b, unit_c):
+            for h in range(2):
+                scatter(span, h)
+        nc.vector.tensor_tensor(place_of(unit_d, 0), t[:, 0, :], sq_s[:, 0, :], ADD)
+        scatter(unit_d, 1)
         for h in range(2):
             nc.sync.dma_start(out[P * h : P * h + P, :], windows[h][:])

@@ -32,6 +32,7 @@ def tile_moe_shr_lin_relu2_kernel(tc, xT, w_words, w_scales, b, gate, offs, out)
     with ExitStack() as ctx:
         held = ctx.enter_context(tc.tile_pool(name="held", bufs=1))
         ring = ctx.enter_context(tc.tile_pool(name="ring", bufs=2))
+        placed = ctx.enter_context(tc.tile_pool(name="placed", bufs=1))
         psum = ctx.enter_context(tc.psum_pool(name="psum", bufs=1))
 
         offsets = held.tile([P, T // 16], U16, name="offsets")
@@ -52,7 +53,10 @@ def tile_moe_shr_lin_relu2_kernel(tc, xT, w_words, w_scales, b, gate, offs, out)
 
         def load_x(a, u):
             for s in range(2):
-                raw = held.tile([P, 2, 512], F32, name=f"raw{a}{u}{s}", align_bytes=64)
+                if s == 0:
+                    raw = held.tile([P, 2, 512], F32, name=f"raw{a}{u}{s}", align_bytes=64)
+                else:
+                    raw = placed.tile([P, 2, 512], F32, name=f"raw{a}{u}{s}", align_bytes=64, offset=2 * T)
                 nc.sync.dma_start(raw[:], x_view[a, u][:, :, 512 * s : 512 * s + 512])
                 raws[a, u, s] = raw
 
@@ -128,13 +132,12 @@ def tile_moe_shr_lin_relu2_kernel(tc, xT, w_words, w_scales, b, gate, offs, out)
         for first in (512, 0):
             gather(0, 0, stage0[:, 0, first : first + 512], first, 512)
         cast(0, 1, shared)
-        for first, count in ((3 * Q, Q), (2 * Q, Q), (0, 2 * Q)):
+        for first, count in ((2 * Q, 2 * Q), (0, 2 * Q)):
             gather(0, 1, stage0[:, 1, first : first + count], first, count)
 
         woven0 = {}
 
-        def weave0(units, name):
-            tile = held.tile([P, 2 * Q * len(units)], U32, name=name, align_bytes=64)
+        def weave0(units, tile):
             for i, q in enumerate(units):
                 woven0[q] = tile[:, 2 * Q * i : 2 * Q * (i + 1)]
                 weave(woven0[q], stage0[:, :, firsts[q] : firsts[q] + Q])
@@ -154,17 +157,18 @@ def tile_moe_shr_lin_relu2_kernel(tc, xT, w_words, w_scales, b, gate, offs, out)
                 weave(woven1[i][:].rearrange("p n u -> p (n u)"), stage1[i])
 
         cast(1, 0, [("S", 0, 160), ("G", 160, 512), ("S", 512, 832), ("G", 832, 1024)])
-        weave0([0], "woven00")
+        weave0([0], held.tile([P, 2 * Q], U32, name="woven00", align_bytes=64))
         for i in range(2):
             woven1[i] = held.tile([P, C, 2], U32, name=f"woven1_{i}", align_bytes=64)
             gather1(0, i)
+        staged = held.tile([P, 2, 3 * Q], U32, name="staged", align_bytes=64)
+        gather(1, 0, staged[:, 0, :], 0, 3 * Q)
         for i in (2, 3, 4):
-            stage1[i] = held.tile([P, 2, Q], U32, name=f"stage1_{i}", align_bytes=64)[:]
-            gather1(0, i)
-        weave0([1], "raw101")
+            stage1[i] = staged[:, :, spans[i][0] : spans[i][0] + Q]
+        weave0([1], held.tile([P, 2 * Q], U32, name="raw101", align_bytes=64))
         cast(1, 1, [("S", 0, 256), ("G", 256, 512), ("S", 512, 832), ("G", 832, 1024)])
-        weave0([2, 3], "raw110")
-        codes0 = held.tile([P, T], U32, name="raw111", align_bytes=64)
+        weave0([2, 3], placed.tile([P, T], U32, name="woven0late", align_bytes=64, offset=4 * T))
+        codes0 = placed.tile([P, T], U32, name="codes0", align_bytes=64, offset=0)
 
         def quantize(a, first, count, words):
             code = codes0[:, first : first + count] if a == 0 else held.tile([P, count], U32, name=f"codes1_{first}", align_bytes=64)[:]
@@ -183,11 +187,13 @@ def tile_moe_shr_lin_relu2_kernel(tc, xT, w_words, w_scales, b, gate, offs, out)
         quantize(0, firsts[0], Q, woven0[0])
         quantize1(0)
         quantize(0, firsts[1], Q, woven0[1])
-        for i in (2, 3, 4):
+        for i in (2, 3):
             gather1(1, i)
             weave1(i, f"woven1_{i}")
         gather1(1, 1)
+        gather1(1, 4)
         quantize1(1)
+        weave1(4, "woven1_4")
         quantize1(2)
         for i in (3, 4):
             quantize(0, firsts[i - 1], Q, woven0[i - 1])
@@ -304,14 +310,18 @@ def tile_moe_shr_lin_relu2_kernel(tc, xT, w_words, w_scales, b, gate, offs, out)
             if name == "d":
                 windows[1] = held.tile([P, T], F32, name="window1", align_bytes=64)
                 scatter(unit_a, 1)
-            t = gated(nc.gpsimd, squares_on_scalar("y" + name, "window1" if name == "c" else f"r_y{name}")[:], span, "t")
+            sq_y = squares_on_scalar("y" + name, "window1" if name == "c" else f"r_y{name}")
             if name != "d":
-                total(nc.gpsimd, span, t, sq_s[:])
-        nc.gpsimd.tensor_tensor(sums[:, 1, 0:Q], t[:, 1, :], sq_s[:, 1, :], ADD)
+                total(nc.gpsimd, span, gated(nc.gpsimd, sq_y[:], span, "t"), sq_s[:])
+        for h in (1, 0):
+            t = held.tile([P, Q], F32, name="t", align_bytes=64)
+            nc.gpsimd.tensor_tensor(t[:], sq_y[:, h, :], weights(*unit_d), MULT)
+            if h == 1:
+                nc.gpsimd.tensor_tensor(sums[:, 1, 0:Q], t[:], sq_s[:, 1, :], ADD)
         for span in (unit_b, unit_c):
             for h in range(2):
                 scatter(span, h)
-        nc.vector.tensor_tensor(place_of(unit_d, 0), t[:, 0, :], sq_s[:, 0, :], ADD)
+        nc.vector.tensor_tensor(place_of(unit_d, 0), t[:], sq_s[:, 0, :], ADD)
         scatter(unit_d, 1)
-        for h in range(2):
+        for h in (1, 0):
             nc.sync.dma_start(out[P * h : P * h + P, :], windows[h][:])

@@ -17,6 +17,7 @@ FP4X4 = mybir.dt.float4_e2m1fn_x4
 ADD = mybir.AluOpType.add
 MULT = mybir.AluOpType.mult
 MAX = mybir.AluOpType.max
+IS_GT = mybir.AluOpType.is_gt
 RELU = mybir.ActivationFunctionType.Relu
 SQUARE = mybir.ActivationFunctionType.Square
 COPY = mybir.ActivationFunctionType.Copy
@@ -205,7 +206,7 @@ def tile_moe_shr_lin_relu2_kernel(tc, xT, w_words, w_scales, b, gate, offs, out)
 
         def passes(a, name, jobs):
             if a == 0:
-                banks[name] = psum.tile([P, 2, Q], F32, name=name)
+                banks[name] = psum.tile([P, 2, Q], F32, name="first" if name == "yd1" else name)
             flat = banks[name][:].rearrange("p j c -> p (j c)")
             col = 0
             for i, (e, h, first, count) in enumerate(jobs):
@@ -228,8 +229,12 @@ def tile_moe_shr_lin_relu2_kernel(tc, xT, w_words, w_scales, b, gate, offs, out)
         jobs = {}
         for name, span in (("first", first_expert), ("second", second_expert)):
             jobs[name] = [(e, h, *span) for e in (span[0] // C, E) for h in range(2)]
-        for name, (first, count) in (("b", unit_b), ("c", unit_c), ("d", unit_d)):
-            jobs["y" + name] = routed(first, 0) + routed(first, 1)
+        for h in range(2):
+            jobs[f"b{h}"] = routed(2 * Q, h) + [(E, h, *unit_b)]
+        jobs["yc"] = routed(Q, 0) + routed(Q, 1)
+        for h in range(2):
+            jobs[f"yd{h}"] = routed(0, h)
+        for name, (first, count) in (("c", unit_c), ("d", unit_d)):
             jobs["s" + name] = [(E, h, first, count) for h in range(2)]
 
         def multiply(a, names):
@@ -239,16 +244,14 @@ def tile_moe_shr_lin_relu2_kernel(tc, xT, w_words, w_scales, b, gate, offs, out)
         def weights(first, count):
             return gates[first // 512][:, first % 512 : first % 512 + count]
 
-        def squares_on_scalar(name, r_name):
+        def squares_on_scalar(name, r_name, sq):
             flat = banks[name][:].rearrange("p j c -> p (j c)")
             r = held.tile([P, 2 * Q], F32, name=r_name, align_bytes=64)
-            sq = held.tile([P, 2, Q], F32, name=f"sq_{name}")
             col = 0
             for e, h, first, count in jobs[name]:
                 nc.scalar.activation(r[:, col : col + count], flat[:, col : col + count], RELU, bias=bias[:, h, e : e + 1])
                 col = col + count
-            nc.scalar.activation(sq[:].rearrange("p j c -> p (j c)"), r[:], SQUARE)
-            return sq
+            nc.scalar.activation(sq.rearrange("p j c -> p (j c)"), r[:, 0:col], SQUARE)
 
         def squares_on_vector(sums, outs, r_names):
             r = [held.tile([P, sums[h].shape[1]], F32, name=r_names[h], align_bytes=64) for h in range(2)]
@@ -269,9 +272,9 @@ def tile_moe_shr_lin_relu2_kernel(tc, xT, w_words, w_scales, b, gate, offs, out)
 
         multiply(0, ("first",))
         multiply(1, ("first",))
-        multiply(0, ("second", "yb", "sb"))
-        multiply(1, ("second", "yb", "sb"))
-        for name in ("yc", "sc", "yd", "sd"):
+        multiply(0, ("second", "b1", "b0"))
+        multiply(1, ("second", "b1", "b0"))
+        for name in ("yc", "sc", "sd", "yd0"):
             for a in range(A):
                 multiply(a, (name,))
 
@@ -287,6 +290,8 @@ def tile_moe_shr_lin_relu2_kernel(tc, xT, w_words, w_scales, b, gate, offs, out)
             total(engine, span, gated(engine, sq[:, 0], span, t_name), sq[:, 1])
 
         single("first", first_expert, nc.vector, "t")
+        for a in range(A):
+            multiply(a, ("yd1",))
         single("second", second_expert, nc.gpsimd, "woven1_4")
         windows = {0: held.tile([P, T], F32, name="pair10", align_bytes=64)}
 
@@ -302,26 +307,63 @@ def tile_moe_shr_lin_relu2_kernel(tc, xT, w_words, w_scales, b, gate, offs, out)
                 nc.scalar.activation(place_of(span, 1), source, COPY)
 
         unit_a = (3 * Q, Q)
-        for name, span in (("b", unit_b), ("c", unit_c), ("d", unit_d)):
-            sq_s = held.tile([P, 2, Q], F32, name=f"sq_s{name}")
-            squares_on_vector([banks["s" + name][:, h, :] for h in range(2)], [sq_s[:, h, :] for h in range(2)], (f"r_s{name}0", f"r_s{name}1"))
+        work = held.tile([P, 5, Q], F32, name="t", align_bytes=64)
+        squares_on_scalar("b1", "r_b1", work[:, 3:5, :])
+        nc.gpsimd.tensor_tensor(work[:, 1, :], work[:, 3, :], weights(*unit_b), MULT)
+        minus_bias = held.tile([P, E], F32, name="pair11", align_bytes=64)
+        nc.vector.tensor_scalar(minus_bias[:], bias[:, 0, 0:E], -1.0, None, MULT)
+
+        def gated_on_vector(bank, span, between, result):
+            kept = held.tile([P, Q], F32, name=f"kept{span[0]}")
+            once = held.tile([P, Q], F32, name=f"once{span[0]}")
+
+            def step(op0, shift, source, target):
+                for j in range(2):
+                    e, cols = span[0] // C + j, slice(C * j, C * j + C)
+                    nc.vector.scalar_tensor_tensor(target[:, cols], bank[:, cols], shift[:, e : e + 1], source[:, cols], op0, MULT)
+
+            step(IS_GT, minus_bias[:], weights(*span), kept[:])
+            step(ADD, bias[:, 0, :], kept[:], once[:])
+            between()
+            step(ADD, bias[:, 0, :], once[:], result())
+
+        r = held.tile([P, Q], F32, name="r_b0")
+        nc.vector.tensor_scalar(r[:], banks["b0"][:, 1, :], bias[:, 0, E : E + 1], 0.0, ADD, MAX)
+        gated_on_vector(
+            banks["b0"][:, 0, :],
+            unit_b,
+            lambda: nc.vector.scalar_tensor_tensor(work[:, 2, :], banks["b0"][:, 1, :], bias[:, 0, E : E + 1], r[:], ADD, MULT),
+            lambda: work[:, 0, :],
+        )
+        nc.gpsimd.tensor_tensor(sums[:, :, 2 * Q : 3 * Q], work[:, 0:2, :], work[:, 2:5:2, :], ADD)
+
+        sq_s = {}
+        for name in ("c", "d"):
+            sq_s[name] = held.tile([P, 2, Q], F32, name=f"sq_s{name}")
+            squares_on_vector([banks["s" + name][:, h, :] for h in range(2)], [sq_s[name][:, h, :] for h in range(2)], (f"r_s{name}0", f"r_s{name}1"))
             if name == "c":
                 scatter(unit_a, 0)
-            if name == "d":
-                windows[1] = held.tile([P, T], F32, name="window1", align_bytes=64)
-                scatter(unit_a, 1)
-            sq_y = squares_on_scalar("y" + name, "window1" if name == "c" else f"r_y{name}")
-            if name != "d":
-                total(nc.gpsimd, span, gated(nc.gpsimd, sq_y[:], span, "t"), sq_s[:])
+        sq_y = held.tile([P, 2, Q], F32, name="sq_yc")
+        squares_on_scalar("yc", "window1", sq_y[:])
+        t = gated(nc.gpsimd, sq_y[:], unit_c, "t")
         for h in (1, 0):
-            t = held.tile([P, Q], F32, name="t", align_bytes=64)
-            nc.gpsimd.tensor_tensor(t[:], sq_y[:, h, :], weights(*unit_d), MULT)
-            if h == 1:
-                nc.gpsimd.tensor_tensor(sums[:, 1, 0:Q], t[:], sq_s[:, 1, :], ADD)
-        for span in (unit_b, unit_c):
-            for h in range(2):
-                scatter(span, h)
-        nc.vector.tensor_tensor(place_of(unit_d, 0), t[:], sq_s[:, 0, :], ADD)
+            nc.gpsimd.tensor_tensor(sums[:, h, Q : 2 * Q], t[:, h, :], sq_s["c"][:, h, :], ADD)
+        windows[1] = held.tile([P, T], F32, name="window1", align_bytes=64)
+        scatter(unit_a, 1)
+        sq_y = held.tile([P, 1, Q], F32, name="sq_yd")
+        squares_on_scalar("yd1", "r_yd", sq_y[:])
+        t = held.tile([P, Q], F32, name="t", align_bytes=64)
+        nc.gpsimd.tensor_tensor(t[:], sq_y[:, 0, :], weights(*unit_d), MULT)
+        nc.gpsimd.tensor_tensor(sums[:, 1, 0:Q], t[:], sq_s["d"][:, 1, :], ADD)
+        t = held.tile([P, Q], F32, name="t", align_bytes=64)
+
+        def middle_scatters():
+            for span in (unit_b, unit_c):
+                for h in range(2):
+                    scatter(span, h)
+
+        gated_on_vector(banks["yd0"][:, 0, :], unit_d, middle_scatters, lambda: t[:])
+        nc.vector.tensor_tensor(place_of(unit_d, 0), t[:], sq_s["d"][:, 0, :], ADD)
         scatter(unit_d, 1)
         for h in (1, 0):
             nc.sync.dma_start(out[P * h : P * h + P, :], windows[h][:])

@@ -26,13 +26,13 @@ P = 128
 A = K // 512
 Q = 256
 NQ = T // Q
+HALF = T // 2
 
 
 def tile_moe_shr_lin_relu2_kernel(tc, xT, w_words, w_scales, b, gate, offs, out):
     nc = tc.nc
     with ExitStack() as ctx:
         held = ctx.enter_context(tc.tile_pool(name="held", bufs=1))
-        ring = ctx.enter_context(tc.tile_pool(name="ring", bufs=2))
         placed = ctx.enter_context(tc.tile_pool(name="placed", bufs=1))
         psum = ctx.enter_context(tc.psum_pool(name="psum", bufs=1))
 
@@ -49,26 +49,16 @@ def tile_moe_shr_lin_relu2_kernel(tc, xT, w_words, w_scales, b, gate, offs, out)
             for i in range(count):
                 s_at[first + i] = (planes[first], i * A)
 
-        x_view = xT.rearrange("(a p u e) n -> a u p e n", p=P, u=2, e=2)
-        raws = {}
+        x_rows = xT.rearrange("(a p t) n -> a t p n", p=P, t=4)
+        rows = {}
 
-        def load_x(a, u):
-            for s in range(2):
-                if s == 0:
-                    raw = held.tile([P, 2, 512], F32, name=f"raw{a}{u}{s}", align_bytes=64)
-                else:
-                    raw = placed.tile([P, 2, 512], F32, name=f"raw{a}{u}{s}", align_bytes=64, offset=2 * T)
-                nc.sync.dma_start(raw[:], x_view[a, u][:, :, 512 * s : 512 * s + 512])
-                raws[a, u, s] = raw
-
-        x_rows = xT.rearrange("(a p u e) n -> a u p (e n)", p=P, u=2, e=2)
-
-        def load_long(a, u):
-            raw = held.tile([P, 2 * T], F32, name=f"raw{a}{u}1", align_bytes=64)
-            nc.sync.dma_start(raw[:, 0 : T + 512], x_rows[a, u][:, 0 : T + 512])
-            nc.sync.dma_start(raw[:, T + 512 : 2 * T], x_rows[a, u][:, T + 512 : 2 * T])
-            for s in range(2):
-                raws[a, u, s] = raw[:].rearrange("p (e n) -> p e n", e=2)[:, :, 512 * s : 512 * s + 512]
+        def load_row(a, t):
+            if (a, t) == (1, 3):
+                row = placed.tile([P, T], F32, name="last_row", align_bytes=64, offset=0)
+            else:
+                row = held.tile([P, T], F32, name=f"row{a}{t}", align_bytes=64)
+            nc.sync.dma_start(row[:], x_rows[a, t])
+            rows[a, t] = row
 
         w_view = w_words.bitcast(I32)
         s_view = w_scales.bitcast(I32)
@@ -87,283 +77,180 @@ def tile_moe_shr_lin_relu2_kernel(tc, xT, w_words, w_scales, b, gate, offs, out)
                 )
 
         bias = held.tile([P, 2, 16], F32, name="bias")
-        gates = [held.tile([P, 512], F32, name=f"gates{i}") for i in range(2)]
+        gates = [held.tile([P, HALF], F32, name=f"gates{i}") for i in range(2)]
 
-        load_long(0, 0)
+        nc.scalar.dma_start(bias[:, :, 0 : E + 1], b.rearrange("(h p) e -> p h e", p=P))
+        load_row(0, 0)
         nc.sync.dma_start(offsets[:], offs)
-        load_long(0, 1)
-        load_long(1, 0)
-        load_x(1, 1)
+        for i in range(1, 4 * A):
+            load_row(i // 4, i % 4)
         load_scales(4, 5)
         load_w(6, 3)
         load_w(4, 2)
-        nc.sync.dma_start(bias[:, :, 0 : E + 1], b.rearrange("(h p) e -> p h e", p=P))
-        nc.sync.dma_start(gates[1][:], gate[0:P, 512:T])
+        nc.sync.dma_start(gates[1][:], gate[0:P, HALF:T])
         load_scales(0, 4)
         load_w(0, 4)
-        nc.sync.dma_start(gates[0][:], gate[0:P, 0:512])
+        nc.sync.dma_start(gates[0][:], gate[0:P, 0:HALF])
 
-        def gpsimd_cast(dst, src):
-            nc.gpsimd.tensor_scalar(dst, src, 1.0, 0.0, MULT, ADD)
+        minus_bias = held.tile([P, 2], F32, name="minus_bias")
+        nc.scalar.activation(minus_bias[:], bias[:, 0, 0:2], COPY, scale=-1.0)
 
-        copies = {"S": nc.scalar.copy, "V": nc.vector.tensor_copy, "G": gpsimd_cast}
+        def picked(a, t, first, count):
+            return rows[a, t][:].indirect(offsets[:, first // 16 : (first + count) // 16])
+
         pairs = {}
+        for a in range(A):
+            upper = held.tile([P, 2, 2, Q, 2], BF16, name=f"upper{a}", align_bytes=64)
+            lower = held.tile([P, 2, HALF, 2], BF16, name=f"lower{a}", align_bytes=64)
+            pairs[a, 0], pairs[a, 1] = upper[:, 1], upper[:, 0]
+            pairs[a, 2], pairs[a, 3] = lower[:, :, Q:HALF, :], lower[:, :, 0:Q, :]
+            for t in range(4):
+                u, e = t // 2, t % 2
+                if t < 3:
+                    nc.vector.tensor_copy(upper[:, :, u, :, e], picked(a, t, HALF, HALF))
+                else:
+                    for q in range(2):
+                        nc.vector.tensor_copy(pairs[a, q][:, u, :, e], picked(a, t, firsts[q], Q))
+                nc.scalar.activation(lower[:, u, :, e], picked(a, t, 0, HALF), COPY)
+            if a == 0:
+                woven0 = held.tile([P, T, 2, 2], BF16, name="woven0", align_bytes=64)
+                for q in range(NQ):
+                    nc.gpsimd.tensor_scalar(woven0[:, firsts[q] : firsts[q] + Q], pairs[0, q].rearrange("p u n e -> p n u e"), 1.0, 0.0, MULT, ADD)
 
-        def cast(a, u, parts):
-            pair = held.tile([P, T, 2], BF16, name=f"pair{a}{u}", align_bytes=64)
-            pairs[a, u] = pair
-            for engine, first, last in parts:
-                at = first % 512
-                copies[engine](pair[:, first:last, :], raws[a, u, first // 512][:, :, at : at + last - first].rearrange("p e n -> p n e"))
+        woven1 = {}
 
-        def gather(a, u, dst, first, count):
-            window = pairs[a, u][:].rearrange("p n e -> p (n e)").bitcast(U32)
-            nc.vector.tensor_copy(dst, window.indirect(offsets[:, first // 16 : (first + count) // 16]))
-
-        def weave(dst, src):
-            nc.scalar.copy(dst.rearrange("p (n u) -> p n u", u=2), src.rearrange("p u n -> p n u"))
+        def weave1(q, engine):
+            woven1[q] = held.tile([P, Q, 2], U32, name=f"woven1_{q}", align_bytes=64)
+            words = pairs[1, q].rearrange("p u n e -> p u (n e)")
+            if engine == "S":
+                nc.scalar.copy(woven1[q][:], words.bitcast(U32).rearrange("p u n -> p n u"))
+            else:
+                nc.vector.tensor_copy(woven1[q][:].bitcast(I32), words.bitcast(I32).rearrange("p u n -> p n u"))
 
         codes = {}
         scales = {}
-
-        shared = [("S", 0, 320), ("G", 320, 512), ("S", 512, 832), ("G", 832, 1024)]
-
-        stage0 = held.tile([P, 2, T], U32, name="stage0", align_bytes=64)
-        cast(0, 0, [("S", 0, 160), ("V", 160, 512), ("S", 512, 672), ("V", 672, 1024)])
-        for first in (512, 0):
-            gather(0, 0, stage0[:, 0, first : first + 512], first, 512)
-        cast(0, 1, shared)
-        for first, count in ((2 * Q, 2 * Q), (0, 2 * Q)):
-            gather(0, 1, stage0[:, 1, first : first + count], first, count)
-
-        woven0 = {}
-
-        def weave0(units, tile):
-            for i, q in enumerate(units):
-                woven0[q] = tile[:, 2 * Q * i : 2 * Q * (i + 1)]
-                weave(woven0[q], stage0[:, :, firsts[q] : firsts[q] + Q])
-
-        spans = [(7 * C, C), (6 * C, C), (2 * Q, Q), (Q, Q), (0, Q)]
-        woven1 = {}
-        stage1 = {}
-
-        def gather1(u, i):
-            gather(1, u, stage1[i][:, u, :] if i in stage1 else woven1[i][:, :, u], *spans[i])
-
-        def weave1(i, name):
-            woven1[i] = held.tile([P, Q, 2], U32, name=name, align_bytes=64)
-            if i == 4:
-                nc.vector.tensor_copy(woven1[i][:].bitcast(I32), stage1[i].bitcast(I32).rearrange("p u n -> p n u"))
-            else:
-                weave(woven1[i][:].rearrange("p n u -> p (n u)"), stage1[i])
-
-        cast(1, 0, [("S", 0, 160), ("G", 160, 512), ("S", 512, 832), ("G", 832, 1024)])
-        weave0([0], held.tile([P, 2 * Q], U32, name="woven00", align_bytes=64))
-        for i in range(2):
-            woven1[i] = held.tile([P, C, 2], U32, name=f"woven1_{i}", align_bytes=64)
-            gather1(0, i)
-        staged = held.tile([P, 2, 3 * Q], U32, name="staged", align_bytes=64)
-        gather(1, 0, staged[:, 0, :], 0, 3 * Q)
-        for i in (2, 3, 4):
-            stage1[i] = staged[:, :, spans[i][0] : spans[i][0] + Q]
-        weave0([1], held.tile([P, 2 * Q], U32, name="raw101", align_bytes=64))
-        cast(1, 1, [("S", 0, 256), ("G", 256, 512), ("S", 512, 832), ("G", 832, 1024)])
-        weave0([2, 3], placed.tile([P, T], U32, name="woven0late", align_bytes=64, offset=4 * T))
         codes0 = placed.tile([P, T], U32, name="codes0", align_bytes=64, offset=0)
 
-        def quantize(a, first, count, words):
+        def quantize(a, first, count, values):
             code = codes0[:, first : first + count] if a == 0 else held.tile([P, count], U32, name=f"codes1_{first}", align_bytes=64)[:]
-            scale = held.tile([P, count], U8, name="woven1_3" if (a, first) == (1, 0) else f"scales{a}_{first}", align_bytes=64)
-            nc.vector.quantize_mx(out=code.bitcast(FP8X4), scales=scale[:], in_=words.bitcast(BF16))
-            codes[a, first, count] = code
-            scales[a, first, count] = scale[:]
-            for at in range(0, count, C):
-                codes[a, first + at, C] = code[:, at : at + C]
-                scales[a, first + at, C] = scale[:, at : at + C]
+            scale = held.tile([P, count], U8, name=f"scales{a}_{first}", align_bytes=64)
+            nc.vector.quantize_mx(out=code.bitcast(FP8X4), scales=scale[:], in_=values)
+            for width in (C, Q):
+                for at in range(0, count, width):
+                    codes[a, first + at, width] = code[:, at : at + width]
+                    scales[a, first + at, width] = scale[:, at : at + width]
 
-        def quantize1(i):
-            quantize(1, *spans[i], woven1[i][:].rearrange("p n u -> p (n u)"))
+        def quantize0(first):
+            quantize(0, first, HALF, woven0[:, first : first + HALF].rearrange("p n u e -> p (n u e)"))
 
-        gather1(1, 0)
-        quantize(0, firsts[0], Q, woven0[0])
+        def quantize1(q):
+            quantize(1, firsts[q], Q, woven1[q][:].rearrange("p n u -> p (n u)").bitcast(BF16))
+
+        for q in range(3):
+            weave1(q, "S")
+        quantize0(HALF)
         quantize1(0)
-        quantize(0, firsts[1], Q, woven0[1])
-        for i in (2, 3):
-            gather1(1, i)
-            weave1(i, f"woven1_{i}")
-        gather1(1, 1)
-        gather1(1, 4)
-        quantize1(1)
-        weave1(4, "woven1_4")
-        quantize1(2)
-        for i in (3, 4):
-            quantize(0, firsts[i - 1], Q, woven0[i - 1])
-            quantize1(i)
-
-        first_expert, second_expert, unit_b, unit_c, unit_d = spans
+        weave1(3, "V")
+        quantize0(0)
+        for q in range(1, NQ):
+            quantize1(q)
 
         banks = {}
+        jobs = {}
+        for q in range(NQ):
+            jobs["routed", q] = [(firsts[q] // C + j, h, firsts[q] + C * j, C) for h in range(2) for j in range(2)]
+            jobs["shared", q] = [(E, h, firsts[q], Q) for h in range(2)]
+        last = NQ - 1
+        by_half = [jobs["routed", last][2 * h : 2 * h + 2] + [jobs["shared", last][h]] for h in range(2)]
+        jobs["routed", last], jobs["shared", last] = by_half[1], by_half[0]
 
-        def passes(a, name, jobs):
+        def passes(a, kind, q):
             if a == 0:
-                banks[name] = psum.tile([P, 2, Q], F32, name="first" if name == "yd1" else name)
-            flat = banks[name][:].rearrange("p j c -> p (j c)")
+                banks[kind, q] = psum.tile([P, 2 * Q], F32, name=f"{kind}{q}")
             col = 0
-            for i, (e, h, first, count) in enumerate(jobs):
+            for i, (e, h, first, count) in enumerate(jobs[kind, q]):
                 words, at = w_at[e]
                 plane, at_s = s_at[e]
                 nc.tensor.matmul_mx(
-                    out=flat[:, col : col + count],
+                    out=banks[kind, q][:, col : col + count],
                     lhsT=words[:, at + a, N * h : N * h + N].bitcast(FP4X4),
                     lhsT_scale=plane[:, at_s + a, P * h : P * h + P],
                     rhs=codes[a, first, count].bitcast(FP8X4),
                     rhs_scale=scales[a, first, count],
                     start=(a == 0 and i == 0),
-                    stop=(a == A - 1 and i == len(jobs) - 1),
+                    stop=(a == A - 1 and i == len(jobs[kind, q]) - 1),
                 )
                 col = col + count
 
-        def routed(first, h):
-            return [(first // C + j, h, first + C * j, C) for j in range(2)]
-
-        jobs = {}
-        for name, span in (("first", first_expert), ("second", second_expert)):
-            jobs[name] = [(e, h, *span) for e in (span[0] // C, E) for h in range(2)]
-        for h in range(2):
-            jobs[f"b{h}"] = routed(2 * Q, h) + [(E, h, *unit_b)]
-        jobs["yc"] = routed(Q, 0) + routed(Q, 1)
-        for h in range(2):
-            jobs[f"yd{h}"] = routed(0, h)
-        for name, (first, count) in (("c", unit_c), ("d", unit_d)):
-            jobs["s" + name] = [(E, h, first, count) for h in range(2)]
-
-        def multiply(a, names):
-            for name in names:
-                passes(a, name, jobs[name])
-
-        def weights(first, count):
-            return gates[first // 512][:, first % 512 : first % 512 + count]
-
-        def squares_on_scalar(name, r_name, sq):
-            flat = banks[name][:].rearrange("p j c -> p (j c)")
-            r = held.tile([P, 2 * Q], F32, name=r_name, align_bytes=64)
-            col = 0
-            for e, h, first, count in jobs[name]:
-                nc.scalar.activation(r[:, col : col + count], flat[:, col : col + count], RELU, bias=bias[:, h, e : e + 1])
-                col = col + count
-            nc.scalar.activation(sq.rearrange("p j c -> p (j c)"), r[:, 0:col], SQUARE)
-
-        def squares_on_vector(sums, outs, r_names):
-            r = [held.tile([P, sums[h].shape[1]], F32, name=r_names[h], align_bytes=64) for h in range(2)]
-            for h in (1, 0):
-                nc.vector.tensor_scalar(r[h][:], sums[h], bias[:, h, E : E + 1], 0.0, ADD, MAX)
-            for h in (1, 0):
-                nc.vector.scalar_tensor_tensor(outs[h], sums[h], bias[:, h, E : E + 1], r[h][:], ADD, MULT)
-
-        sums = held.tile([P, 2, T], F32, name="sums", align_bytes=64)
-
-        def gated(engine, sq, span, name):
-            t = held.tile([P, 2, span[1]], F32, name=name, align_bytes=64)
-            engine.tensor_tensor(t[:], sq, weights(*span).unsqueeze(1).to_broadcast([P, 2, span[1]]), MULT)
-            return t
-
-        def total(engine, span, t, sq_s):
-            engine.tensor_tensor(sums[:, :, span[0] : span[0] + span[1]], t[:], sq_s, ADD)
-
-        multiply(0, ("first",))
-        multiply(1, ("first",))
-        multiply(0, ("second", "b1", "b0"))
-        multiply(1, ("second", "b1", "b0"))
-        for name in ("yc", "sc", "sd", "yd0"):
+        order = [(kind, q) for q in range(2) for kind in ("routed", "shared")] + [("routed", 2), ("shared", last), ("shared", 2), ("routed", last)]
+        for kind, q in order:
             for a in range(A):
-                multiply(a, (name,))
+                passes(a, kind, q)
 
-        def single(name, span, engine, t_name):
-            bank = banks[name][:].rearrange("p j (h c) -> p j h c", h=2)
-            sq = held.tile([P, 2, 2, C], F32, name=f"sq_{name}")
-            for j in range(2):
-                r = ring.tile([P, 2, C], F32, name="r")
-                e = jobs[name][2 * j][0]
-                for h in range(2):
-                    nc.scalar.activation(r[:, h, :], bank[:, j, h, :], RELU, bias=bias[:, h, e : e + 1])
-                nc.scalar.activation(sq[:, j], r[:], SQUARE)
-            total(engine, span, gated(engine, sq[:, 0], span, t_name), sq[:, 1])
+        def squares_on_scalar(bank, parts, r_name, sq):
+            r = held.tile([P, sq.shape[1]], F32, name=r_name, align_bytes=64)
+            col = 0
+            for e, h, first, count in parts:
+                nc.scalar.activation(r[:, col : col + count], bank[:, col : col + count], RELU, bias=bias[:, h, e : e + 1])
+                col = col + count
+            nc.scalar.activation(sq, r[:], SQUARE)
 
-        single("first", first_expert, nc.vector, "t")
-        for a in range(A):
-            multiply(a, ("yd1",))
-        single("second", second_expert, nc.gpsimd, "woven1_4")
-        windows = {0: held.tile([P, T], F32, name="pair10", align_bytes=64)}
+        def squares_on_vector(q, halves, r_name, sq):
+            r = held.tile([P, 2, Q], F32, name=r_name, align_bytes=64)
+            bank = banks["shared", q]
+            for h in halves:
+                nc.vector.tensor_scalar(r[:, h, :], bank[:, Q * h : Q * h + Q], bias[:, h, E : E + 1], 0.0, ADD, MAX)
+            for h in halves:
+                nc.vector.scalar_tensor_tensor(sq[:, h, :], bank[:, Q * h : Q * h + Q], bias[:, h, E : E + 1], r[:, h, :], ADD, MULT)
 
-        def place_of(span, h):
-            first, count = span
-            return windows[h][:].indirect(offsets[:, first // 16 : (first + count) // 16])
-
-        def scatter(span, h):
-            source = sums[:, h, span[0] : span[0] + span[1]]
-            if h == 0:
-                nc.vector.tensor_copy(place_of(span, 0), source)
-            else:
-                nc.scalar.activation(place_of(span, 1), source, COPY)
-
-        unit_a = (3 * Q, Q)
-        work = held.tile([P, 5, Q], F32, name="t", align_bytes=64)
-        squares_on_scalar("b1", "r_b1", work[:, 3:5, :])
-        nc.gpsimd.tensor_tensor(work[:, 1, :], work[:, 3, :], weights(*unit_b), MULT)
-        minus_bias = held.tile([P, E], F32, name="pair11", align_bytes=64)
-        nc.vector.tensor_scalar(minus_bias[:], bias[:, 0, 0:E], -1.0, None, MULT)
-
-        def gated_on_vector(bank, span, between, result):
-            kept = held.tile([P, Q], F32, name=f"kept{span[0]}")
-            once = held.tile([P, Q], F32, name=f"once{span[0]}")
+        def last_half_on_vector(steps):
+            bank = banks["shared", last]
 
             def step(op0, shift, source, target):
                 for j in range(2):
-                    e, cols = span[0] // C + j, slice(C * j, C * j + C)
-                    nc.vector.scalar_tensor_tensor(target[:, cols], bank[:, cols], shift[:, e : e + 1], source[:, cols], op0, MULT)
+                    cols = slice(C * j, C * j + C)
+                    nc.vector.scalar_tensor_tensor(target[:, cols], bank[:, cols], shift[:, j : j + 1], source[:, cols], op0, MULT)
 
-            step(IS_GT, minus_bias[:], weights(*span), kept[:])
-            step(ADD, bias[:, 0, :], kept[:], once[:])
-            between()
-            step(ADD, bias[:, 0, :], once[:], result())
+            step(IS_GT, minus_bias[:], gates[0][:, 0:Q], steps[:, 0, :])
+            nc.vector.tensor_scalar(steps[:, 3, :], bank[:, Q : 2 * Q], bias[:, 0, E : E + 1], 0.0, ADD, MAX)
+            step(ADD, bias[:, 0, :], steps[:, 0, :], steps[:, 1, :])
+            nc.vector.scalar_tensor_tensor(steps[:, 4, :], bank[:, Q : 2 * Q], bias[:, 0, E : E + 1], steps[:, 3, :], ADD, MULT)
+            step(ADD, bias[:, 0, :], steps[:, 1, :], steps[:, 2, :])
 
-        r = held.tile([P, Q], F32, name="r_b0")
-        nc.vector.tensor_scalar(r[:], banks["b0"][:, 1, :], bias[:, 0, E : E + 1], 0.0, ADD, MAX)
-        gated_on_vector(
-            banks["b0"][:, 0, :],
-            unit_b,
-            lambda: nc.vector.scalar_tensor_tensor(work[:, 2, :], banks["b0"][:, 1, :], bias[:, 0, E : E + 1], r[:], ADD, MULT),
-            lambda: work[:, 0, :],
-        )
-        nc.gpsimd.tensor_tensor(sums[:, :, 2 * Q : 3 * Q], work[:, 0:2, :], work[:, 2:5:2, :], ADD)
+        sums = {}
+        steps = held.tile([P, 5, Q], F32, name="steps", align_bytes=64)
+        for q in range(last):
+            routed = held.tile([P, 2, Q], F32, name=f"routed{q}", align_bytes=64)
+            shared = held.tile([P, 2, Q], F32, name=f"shared{q}", align_bytes=64)
+            squares_on_scalar(banks["routed", q], jobs["routed", q], f"r_routed{q}", routed[:].rearrange("p h c -> p (h c)"))
+            if q == 0:
+                squares_on_scalar(banks["shared", q][:, Q : 2 * Q], jobs["shared", q][1:], "r_first", shared[:, 1, :])
+            if q == last - 1:
+                last_half_on_vector(steps)
+            squares_on_vector(q, (0,) if q == 0 else (0, 1), "window0" if q == last - 1 else f"r_shared{q}", shared)
+            gated = held.tile([P, 2, Q], F32, name="woven1_3" if q == 0 else f"gated{q}", align_bytes=64)
+            weights = gates[firsts[q] // HALF][:, firsts[q] % HALF : firsts[q] % HALF + Q]
+            nc.gpsimd.tensor_tensor(gated[:], routed[:], weights.unsqueeze(1).to_broadcast([P, 2, Q]), MULT)
+            sums[q] = held.tile([P, 2, Q], F32, name=f"sums{q}", align_bytes=64)
+            nc.gpsimd.tensor_tensor(sums[q][:], gated[:], shared[:], ADD)
 
-        sq_s = {}
-        for name in ("c", "d"):
-            sq_s[name] = held.tile([P, 2, Q], F32, name=f"sq_s{name}")
-            squares_on_vector([banks["s" + name][:, h, :] for h in range(2)], [sq_s[name][:, h, :] for h in range(2)], (f"r_s{name}0", f"r_s{name}1"))
-            if name == "c":
-                scatter(unit_a, 0)
-        sq_y = held.tile([P, 2, Q], F32, name="sq_yc")
-        squares_on_scalar("yc", "window1", sq_y[:])
-        t = gated(nc.gpsimd, sq_y[:], unit_c, "t")
-        for h in (1, 0):
-            nc.gpsimd.tensor_tensor(sums[:, h, Q : 2 * Q], t[:, h, :], sq_s["c"][:, h, :], ADD)
-        windows[1] = held.tile([P, T], F32, name="window1", align_bytes=64)
-        scatter(unit_a, 1)
-        sq_y = held.tile([P, 1, Q], F32, name="sq_yd")
-        squares_on_scalar("yd1", "r_yd", sq_y[:])
-        t = held.tile([P, Q], F32, name="t", align_bytes=64)
-        nc.gpsimd.tensor_tensor(t[:], sq_y[:, 0, :], weights(*unit_d), MULT)
-        nc.gpsimd.tensor_tensor(sums[:, 1, 0:Q], t[:], sq_s["d"][:, 1, :], ADD)
-        t = held.tile([P, Q], F32, name="t", align_bytes=64)
+        both = held.tile([P, 2, Q], F32, name="both", align_bytes=64)
+        squares_on_scalar(banks["routed", last], jobs["routed", last], "window1", both[:].rearrange("p j c -> p (j c)"))
+        ends = held.tile([P, 2, Q], F32, name="ends", align_bytes=64)
+        nc.gpsimd.tensor_tensor(ends[:, 0, :], both[:, 0, :], gates[0][:, 0:Q], MULT)
+        nc.gpsimd.tensor_tensor(ends[:, 1, :], ends[:, 0, :], both[:, 1, :], ADD)
 
-        def middle_scatters():
-            for span in (unit_b, unit_c):
-                for h in range(2):
-                    scatter(span, h)
+        windows = [held.tile([P, T], F32, name=f"window{h}", align_bytes=64) for h in range(2)]
 
-        gated_on_vector(banks["yd0"][:, 0, :], unit_d, middle_scatters, lambda: t[:])
-        nc.vector.tensor_tensor(place_of(unit_d, 0), t[:], sq_s["d"][:, 0, :], ADD)
-        scatter(unit_d, 1)
-        for h in (1, 0):
+        def place_of(q, h):
+            return windows[h][:].indirect(offsets[:, firsts[q] // 16 : (firsts[q] + Q) // 16])
+
+        for q in range(NQ):
+            if q < last:
+                nc.vector.tensor_copy(place_of(q, 0), sums[q][:, 0, :])
+                nc.scalar.activation(place_of(q, 1), sums[q][:, 1, :], COPY)
+            else:
+                nc.vector.tensor_tensor(place_of(q, 0), steps[:, 2, :], steps[:, 4, :], ADD)
+                nc.scalar.activation(place_of(q, 1), ends[:, 1, :], COPY)
+        for h in range(2):
             nc.sync.dma_start(out[P * h : P * h + P, :], windows[h][:])

@@ -33,7 +33,6 @@ def tile_moe_shr_lin_relu2_kernel(tc, xT, w_words, w_scales, b, gate, offs, out)
     nc = tc.nc
     with ExitStack() as ctx:
         held = ctx.enter_context(tc.tile_pool(name="held", bufs=1))
-        placed = ctx.enter_context(tc.tile_pool(name="placed", bufs=1))
         psum = ctx.enter_context(tc.psum_pool(name="psum", bufs=1))
 
         offsets = held.tile([P, T // 16], U16, name="offsets")
@@ -53,10 +52,7 @@ def tile_moe_shr_lin_relu2_kernel(tc, xT, w_words, w_scales, b, gate, offs, out)
         rows = {}
 
         def load_row(a, t):
-            if (a, t) == (1, 3):
-                row = placed.tile([P, T], F32, name="last_row", align_bytes=64, offset=0)
-            else:
-                row = held.tile([P, T], F32, name=f"row{a}{t}", align_bytes=64)
+            row = held.tile([P, T], F32, name=f"row{a}{t}", align_bytes=64)
             nc.sync.dma_start(row[:], x_rows[a, t])
             rows[a, t] = row
 
@@ -70,10 +66,10 @@ def tile_moe_shr_lin_relu2_kernel(tc, xT, w_words, w_scales, b, gate, offs, out)
                 w_at[first + i] = (tile, i * A)
 
         def load_scales(first, count):
-            for quad in range(4):
+            for r in range(4):
                 nc.sync.dma_start(
-                    planes[first][32 * quad : 32 * quad + 4].bitcast(I32),
-                    s_view[first : first + count, :, 4 * quad : 4 * quad + 4, :].rearrange("e a q n -> q (e a) n"),
+                    planes[first][r:P:32].bitcast(I32),
+                    s_view[first : first + count, :, r:16:4, :].rearrange("e a q n -> q (e a) n"),
                 )
 
         bias = held.tile([P, 2, 16], F32, name="bias")
@@ -92,47 +88,71 @@ def tile_moe_shr_lin_relu2_kernel(tc, xT, w_words, w_scales, b, gate, offs, out)
         load_w(0, 4)
         nc.sync.dma_start(gates[0][:], gate[0:P, 0:HALF])
 
+        split = 2
+        last = NQ - 1
         minus_bias = held.tile([P, 2], F32, name="minus_bias")
-        nc.scalar.activation(minus_bias[:], bias[:, 0, 0:2], COPY, scale=-1.0)
+        nc.scalar.activation(minus_bias[:], bias[:, 0, firsts[split] // C : firsts[split] // C + 2], COPY, scale=-1.0)
 
         def picked(a, t, first, count):
             return rows[a, t][:].indirect(offsets[:, first // 16 : (first + count) // 16])
 
-        pairs = {}
-        for a in range(A):
-            upper = held.tile([P, 2, 2, Q, 2], BF16, name=f"upper{a}", align_bytes=64)
-            lower = held.tile([P, 2, HALF, 2], BF16, name=f"lower{a}", align_bytes=64)
-            pairs[a, 0], pairs[a, 1] = upper[:, 1], upper[:, 0]
-            pairs[a, 2], pairs[a, 3] = lower[:, :, Q:HALF, :], lower[:, :, 0:Q, :]
-            for t in range(4):
-                u, e = t // 2, t % 2
-                if t < 3:
-                    nc.vector.tensor_copy(upper[:, :, u, :, e], picked(a, t, HALF, HALF))
-                else:
-                    for q in range(2):
-                        nc.vector.tensor_copy(pairs[a, q][:, u, :, e], picked(a, t, firsts[q], Q))
-                nc.scalar.activation(lower[:, u, :, e], picked(a, t, 0, HALF), COPY)
-            if a == 0:
-                woven0 = held.tile([P, T, 2, 2], BF16, name="woven0", align_bytes=64)
-                for q in range(NQ):
-                    nc.gpsimd.tensor_scalar(woven0[:, firsts[q] : firsts[q] + Q], pairs[0, q].rearrange("p u n e -> p n u e"), 1.0, 0.0, MULT, ADD)
+        def on_vector(dst, a, t, first, count):
+            nc.vector.tensor_copy(dst, picked(a, t, first, count))
 
-        woven1 = {}
+        def on_scalar(dst, a, t, first, count):
+            nc.scalar.activation(dst, picked(a, t, first, count), COPY)
 
-        def weave1(q, engine):
-            woven1[q] = held.tile([P, Q, 2], U32, name=f"woven1_{q}", align_bytes=64)
-            words = pairs[1, q].rearrange("p u n e -> p u (n e)")
-            if engine == "S":
-                nc.scalar.copy(woven1[q][:], words.bitcast(U32).rearrange("p u n -> p n u"))
+        upper0 = held.tile([P, 2, 2, Q, 2], BF16, name="upper0", align_bytes=64)
+        lower0 = held.tile([P, 2, HALF, 2], BF16, name="lower0", align_bytes=64)
+        for t in range(4):
+            u, e = t // 2, t % 2
+            if t < 3:
+                on_vector(upper0[:, :, u, :, e], 0, t, HALF, HALF)
             else:
-                nc.vector.tensor_copy(woven1[q][:].bitcast(I32), words.bitcast(I32).rearrange("p u n -> p n u"))
+                for q in range(2):
+                    on_vector(upper0[:, 1 - q, u, :, e], 0, t, firsts[q], Q)
+            on_scalar(lower0[:, u, :, e], 0, t, 0, HALF)
+        woven0 = held.tile([P, T, 2, 2], BF16, name="woven0", align_bytes=64)
+        for source, first, count in ((upper0[:, 1], 3 * Q, Q), (lower0[:, :, Q:HALF, :], Q, Q), (lower0[:, :, C:Q, :], C, C), (upper0[:, 0], HALF, Q)):
+            nc.gpsimd.tensor_scalar(woven0[:, first : first + count], source.rearrange("p u n e -> p n u e"), 1.0, 0.0, MULT, ADD)
+        nc.scalar.copy(
+            woven0[:, 0:C].rearrange("p n u e -> p n (u e)").bitcast(U32),
+            lower0[:, :, 0:C, :].rearrange("p u n e -> p u (n e)").bitcast(U32).rearrange("p u n -> p n u"),
+        )
+
+        upper1 = held.tile([P, 4, 2, C, 2], BF16, name="upper1", align_bytes=64)
+        lower1 = held.tile([P, 2, HALF, 2], BF16, name="lower1", align_bytes=64)
+        for t in range(4):
+            u, e = t // 2, t % 2
+            if t < 2:
+                on_vector(upper1[:, :, u, :, e], 1, t, HALF, HALF)
+            elif t == 2:
+                on_vector(upper1[:, 1:4, u, :, e], 1, t, HALF + C, 3 * C)
+            else:
+                on_vector(upper1[:, 2:4, u, :, e], 1, t, 3 * Q, Q)
+                on_vector(upper1[:, 1, u, :, e], 1, t, HALF + C, C)
+            on_scalar(lower1[:, u, :, e], 1, t, 0, HALF)
+            if t >= 2:
+                on_scalar(upper1[:, 0, u, :, e], 1, t, HALF, C)
+
+        woven1 = {first: held.tile([P, count, 2], U32, name=f"woven1_{first}", align_bytes=64) for first, count in ((3 * Q, Q), (HALF, Q), (0, HALF))}
+
+        def upper_words(first, dtype):
+            j = (first - HALF) // C
+            source = upper1[:, j : j + 2].rearrange("p j u n e -> p j u (n e)").bitcast(dtype).rearrange("p j u n -> p j n u")
+            return woven1[first][:].bitcast(dtype).rearrange("p (j n) u -> p j n u", j=2), source
 
         codes = {}
         scales = {}
-        codes0 = placed.tile([P, T], U32, name="codes0", align_bytes=64, offset=0)
+        codes0 = held.tile([P, T], U32, name="upper0", align_bytes=64)
 
-        def quantize(a, first, count, values):
-            code = codes0[:, first : first + count] if a == 0 else held.tile([P, count], U32, name=f"codes1_{first}", align_bytes=64)[:]
+        def quantize(a, first, count):
+            if a == 0:
+                code = codes0[:, first : first + count]
+                values = woven0[:, first : first + count].rearrange("p n u e -> p (n u e)")
+            else:
+                code = held.tile([P, count], U32, name=f"codes1_{first}", align_bytes=64)[:]
+                values = woven1[first][:].rearrange("p n u -> p (n u)").bitcast(BF16)
             scale = held.tile([P, count], U8, name=f"scales{a}_{first}", align_bytes=64)
             nc.vector.quantize_mx(out=code.bitcast(FP8X4), scales=scale[:], in_=values)
             for width in (C, Q):
@@ -140,29 +160,23 @@ def tile_moe_shr_lin_relu2_kernel(tc, xT, w_words, w_scales, b, gate, offs, out)
                     codes[a, first + at, width] = code[:, at : at + width]
                     scales[a, first + at, width] = scale[:, at : at + width]
 
-        def quantize0(first):
-            quantize(0, first, HALF, woven0[:, first : first + HALF].rearrange("p n u e -> p (n u e)"))
-
-        def quantize1(q):
-            quantize(1, firsts[q], Q, woven1[q][:].rearrange("p n u -> p (n u)").bitcast(BF16))
-
-        for q in range(3):
-            weave1(q, "S")
-        quantize0(HALF)
-        quantize1(0)
-        weave1(3, "V")
-        quantize0(0)
-        for q in range(1, NQ):
-            quantize1(q)
+        nc.vector.tensor_copy(*upper_words(3 * Q, I32))
+        nc.scalar.copy(*upper_words(HALF, U32))
+        quantize(0, 3 * Q, Q)
+        quantize(1, 3 * Q, Q)
+        quantize(0, HALF, Q)
+        quantize(0, 0, HALF)
+        nc.vector.tensor_copy(woven1[0][:].bitcast(I32), lower1[:].rearrange("p u n e -> p u (n e)").bitcast(I32).rearrange("p u n -> p n u"))
+        quantize(1, HALF, Q)
+        quantize(1, 0, HALF)
 
         banks = {}
         jobs = {}
         for q in range(NQ):
             jobs["routed", q] = [(firsts[q] // C + j, h, firsts[q] + C * j, C) for h in range(2) for j in range(2)]
             jobs["shared", q] = [(E, h, firsts[q], Q) for h in range(2)]
-        last = NQ - 1
-        by_half = [jobs["routed", last][2 * h : 2 * h + 2] + [jobs["shared", last][h]] for h in range(2)]
-        jobs["routed", last], jobs["shared", last] = by_half[1], by_half[0]
+        by_half = [jobs["routed", split][2 * h : 2 * h + 2] + [jobs["shared", split][h]] for h in range(2)]
+        jobs["routed", split], jobs["shared", split] = by_half[1], by_half[0]
 
         def passes(a, kind, q):
             if a == 0:
@@ -182,10 +196,10 @@ def tile_moe_shr_lin_relu2_kernel(tc, xT, w_words, w_scales, b, gate, offs, out)
                 )
                 col = col + count
 
-        order = [(kind, q) for q in range(2) for kind in ("routed", "shared")] + [("routed", 2), ("shared", last), ("shared", 2), ("routed", last)]
-        for kind, q in order:
-            for a in range(A):
-                passes(a, kind, q)
+        for q in range(NQ):
+            for kind in ("routed", "shared"):
+                for a in range(A):
+                    passes(a, kind, q)
 
         def squares_on_scalar(bank, parts, r_name, sq):
             r = held.tile([P, sq.shape[1]], F32, name=r_name, align_bytes=64)
@@ -195,62 +209,75 @@ def tile_moe_shr_lin_relu2_kernel(tc, xT, w_words, w_scales, b, gate, offs, out)
                 col = col + count
             nc.scalar.activation(sq, r[:], SQUARE)
 
-        def squares_on_vector(q, halves, r_name, sq):
-            r = held.tile([P, 2, Q], F32, name=r_name, align_bytes=64)
+        def squares_on_vector(q, halves, r, sq):
             bank = banks["shared", q]
             for h in halves:
                 nc.vector.tensor_scalar(r[:, h, :], bank[:, Q * h : Q * h + Q], bias[:, h, E : E + 1], 0.0, ADD, MAX)
             for h in halves:
                 nc.vector.scalar_tensor_tensor(sq[:, h, :], bank[:, Q * h : Q * h + Q], bias[:, h, E : E + 1], r[:, h, :], ADD, MULT)
 
-        def last_half_on_vector(steps):
-            bank = banks["shared", last]
+        def weights(q):
+            return gates[firsts[q] // HALF][:, firsts[q] % HALF : firsts[q] % HALF + Q]
+
+        def half_on_vector(q, gated, shared):
+            bank = banks["shared", q]
+            e = firsts[q] // C
 
             def step(op0, shift, source, target):
                 for j in range(2):
                     cols = slice(C * j, C * j + C)
                     nc.vector.scalar_tensor_tensor(target[:, cols], bank[:, cols], shift[:, j : j + 1], source[:, cols], op0, MULT)
 
-            step(IS_GT, minus_bias[:], gates[0][:, 0:Q], steps[:, 0, :])
-            nc.vector.tensor_scalar(steps[:, 3, :], bank[:, Q : 2 * Q], bias[:, 0, E : E + 1], 0.0, ADD, MAX)
-            step(ADD, bias[:, 0, :], steps[:, 0, :], steps[:, 1, :])
-            nc.vector.scalar_tensor_tensor(steps[:, 4, :], bank[:, Q : 2 * Q], bias[:, 0, E : E + 1], steps[:, 3, :], ADD, MULT)
-            step(ADD, bias[:, 0, :], steps[:, 1, :], steps[:, 2, :])
+            step(IS_GT, minus_bias[:], weights(q), steps[:, 0, :])
+            nc.vector.tensor_scalar(steps[:, 2, :], bank[:, Q : 2 * Q], bias[:, 0, E : E + 1], 0.0, ADD, MAX)
+            step(ADD, bias[:, 0, e : e + 2], steps[:, 0, :], steps[:, 1, :])
+            nc.vector.scalar_tensor_tensor(shared, bank[:, Q : 2 * Q], bias[:, 0, E : E + 1], steps[:, 2, :], ADD, MULT)
+            step(ADD, bias[:, 0, e : e + 2], steps[:, 1, :], gated)
 
+        windows = {}
         sums = {}
-        steps = held.tile([P, 5, Q], F32, name="steps", align_bytes=64)
-        for q in range(last):
-            routed = held.tile([P, 2, Q], F32, name=f"routed{q}", align_bytes=64)
-            shared = held.tile([P, 2, Q], F32, name=f"shared{q}", align_bytes=64)
-            squares_on_scalar(banks["routed", q], jobs["routed", q], f"r_routed{q}", routed[:].rearrange("p h c -> p (h c)"))
-            if q == 0:
-                squares_on_scalar(banks["shared", q][:, Q : 2 * Q], jobs["shared", q][1:], "r_first", shared[:, 1, :])
-            if q == last - 1:
-                last_half_on_vector(steps)
-            squares_on_vector(q, (0,) if q == 0 else (0, 1), "window0" if q == last - 1 else f"r_shared{q}", shared)
-            gated = held.tile([P, 2, Q], F32, name="woven1_3" if q == 0 else f"gated{q}", align_bytes=64)
-            weights = gates[firsts[q] // HALF][:, firsts[q] % HALF : firsts[q] % HALF + Q]
-            nc.gpsimd.tensor_tensor(gated[:], routed[:], weights.unsqueeze(1).to_broadcast([P, 2, Q]), MULT)
-            sums[q] = held.tile([P, 2, Q], F32, name=f"sums{q}", align_bytes=64)
-            nc.gpsimd.tensor_tensor(sums[q][:], gated[:], shared[:], ADD)
-
-        both = held.tile([P, 2, Q], F32, name="both", align_bytes=64)
-        squares_on_scalar(banks["routed", last], jobs["routed", last], "window1", both[:].rearrange("p j c -> p (j c)"))
-        ends = held.tile([P, 2, Q], F32, name="ends", align_bytes=64)
-        nc.gpsimd.tensor_tensor(ends[:, 0, :], both[:, 0, :], gates[0][:, 0:Q], MULT)
-        nc.gpsimd.tensor_tensor(ends[:, 1, :], ends[:, 0, :], both[:, 1, :], ADD)
-
-        windows = [held.tile([P, T], F32, name=f"window{h}", align_bytes=64) for h in range(2)]
 
         def place_of(q, h):
             return windows[h][:].indirect(offsets[:, firsts[q] // 16 : (firsts[q] + Q) // 16])
 
-        for q in range(NQ):
-            if q < last:
+        def scatter(q, h):
+            if h == 0:
                 nc.vector.tensor_copy(place_of(q, 0), sums[q][:, 0, :])
-                nc.scalar.activation(place_of(q, 1), sums[q][:, 1, :], COPY)
             else:
-                nc.vector.tensor_tensor(place_of(q, 0), steps[:, 2, :], steps[:, 4, :], ADD)
-                nc.scalar.activation(place_of(q, 1), ends[:, 1, :], COPY)
-        for h in range(2):
+                nc.scalar.activation(place_of(q, 1), sums[q][:, 1, :], COPY)
+
+        for q in range(NQ):
+            sums[q] = held.tile([P, 2, Q], F32, name=f"sums{q}", align_bytes=64)
+            if q == split:
+                parts = held.tile([P, 5, Q], F32, name="parts", align_bytes=64)
+                steps = held.tile([P, 3, Q], F32, name="window0", align_bytes=64)
+                squares_on_scalar(banks["routed", q], jobs["routed", q], "window1", parts[:, 3:5, :].rearrange("p j c -> p (j c)"))
+                half_on_vector(q, parts[:, 0, :], parts[:, 2, :])
+                nc.gpsimd.tensor_tensor(parts[:, 1, :], parts[:, 3, :], weights(q), MULT)
+                nc.gpsimd.tensor_tensor(sums[q][:], parts[:, 0:2, :], parts[:, 2:5:2, :], ADD)
+                for h in range(2):
+                    windows[h] = held.tile([P, T], F32, name=f"window{h}", align_bytes=64)
+                    scatter(0, h)
+                continue
+            routed = held.tile([P, 2, Q], F32, name=f"routed{q}", align_bytes=64)
+            shared = held.tile([P, 2, Q], F32, name=f"shared{q}", align_bytes=64)
+            squares_on_scalar(banks["routed", q], jobs["routed", q], f"r_routed{q}", routed[:].rearrange("p h c -> p (h c)"))
+            squares_on_vector(q, (1, 0), held.tile([P, 2, Q], F32, name=f"r_shared{q}", align_bytes=64), shared)
+            if q < last:
+                gated = held.tile([P, 2, Q], F32, name="woven1_0" if q == 0 else f"gated{q}", align_bytes=64)
+                nc.gpsimd.tensor_tensor(gated[:], routed[:], weights(q).unsqueeze(1).to_broadcast([P, 2, Q]), MULT)
+                nc.gpsimd.tensor_tensor(sums[q][:], gated[:], shared[:], ADD)
+            else:
+                gated = held.tile([P, Q], F32, name="gated_last", align_bytes=64)
+                nc.gpsimd.tensor_tensor(gated[:], routed[:, 1, :], weights(q), MULT)
+                nc.gpsimd.tensor_tensor(sums[q][:, 1, :], gated[:], shared[:, 1, :], ADD)
+                gated = held.tile([P, Q], F32, name="gated_last", align_bytes=64)
+                nc.gpsimd.tensor_tensor(gated[:], routed[:, 0, :], weights(q), MULT)
+
+        for q in range(1, last):
+            for h in range(2):
+                scatter(q, h)
+        scatter(last, 1)
+        nc.vector.tensor_tensor(place_of(last, 0), gated[:], shared[:, 0, :], ADD)
+        for h in (1, 0):
             nc.sync.dma_start(out[P * h : P * h + P, :], windows[h][:])

@@ -85,8 +85,9 @@ def tile_moe_shr_lin_relu2_kernel(tc, xT, w_words, w_scales, b, gate, offs, out)
         load_w(4, 2)
         nc.sync.dma_start(gates[1][:], gate[0:P, HALF:T])
         load_scales(0, 4)
-        load_w(0, 4)
+        load_w(2, 2)
         nc.sync.dma_start(gates[0][:], gate[0:P, 0:HALF])
+        load_w(0, 2)
 
         split = 2
         last = NQ - 1
@@ -113,34 +114,28 @@ def tile_moe_shr_lin_relu2_kernel(tc, xT, w_words, w_scales, b, gate, offs, out)
                     on_vector(upper0[:, 1 - q, u, :, e], 0, t, firsts[q], Q)
             on_scalar(lower0[:, u, :, e], 0, t, 0, HALF)
         woven0 = held.tile([P, T, 2, 2], BF16, name="woven0", align_bytes=64)
-        for source, first, count in ((upper0[:, 1], 3 * Q, Q), (lower0[:, :, Q:HALF, :], Q, Q), (lower0[:, :, C:Q, :], C, C), (upper0[:, 0], HALF, Q)):
-            nc.gpsimd.tensor_scalar(woven0[:, first : first + count], source.rearrange("p u n e -> p n u e"), 1.0, 0.0, MULT, ADD)
-        nc.scalar.copy(
-            woven0[:, 0:C].rearrange("p n u e -> p n (u e)").bitcast(U32),
-            lower0[:, :, 0:C, :].rearrange("p u n e -> p u (n e)").bitcast(U32).rearrange("p u n -> p n u"),
-        )
+        for source, first in ((upper0[:, 1], 3 * Q), (lower0[:, :, Q:HALF, :], Q), (lower0[:, :, 0:Q, :], 0)):
+            nc.gpsimd.tensor_scalar(woven0[:, first : first + Q], source.rearrange("p u n e -> p n u e"), 1.0, 0.0, MULT, ADD)
 
-        upper1 = held.tile([P, 4, 2, C, 2], BF16, name="upper1", align_bytes=64)
+        upper1 = held.tile([P, 2, 2, Q, 2], BF16, name="upper1", align_bytes=64)
         lower1 = held.tile([P, 2, HALF, 2], BF16, name="lower1", align_bytes=64)
         for t in range(4):
             u, e = t // 2, t % 2
             if t < 2:
                 on_vector(upper1[:, :, u, :, e], 1, t, HALF, HALF)
-            elif t == 2:
-                on_vector(upper1[:, 1:4, u, :, e], 1, t, HALF + C, 3 * C)
             else:
-                on_vector(upper1[:, 2:4, u, :, e], 1, t, 3 * Q, Q)
-                on_vector(upper1[:, 1, u, :, e], 1, t, HALF + C, C)
+                on_vector(upper1[:, 1, u, :, e], 1, t, 3 * Q, Q)
+                on_scalar(upper1[:, 0, u, :, e], 1, t, HALF, Q)
             on_scalar(lower1[:, u, :, e], 1, t, 0, HALF)
-            if t >= 2:
-                on_scalar(upper1[:, 0, u, :, e], 1, t, HALF, C)
 
         woven1 = {first: held.tile([P, count, 2], U32, name=f"woven1_{first}", align_bytes=64) for first, count in ((3 * Q, Q), (HALF, Q), (0, HALF))}
 
-        def upper_words(first, dtype):
-            j = (first - HALF) // C
-            source = upper1[:, j : j + 2].rearrange("p j u n e -> p j u (n e)").bitcast(dtype).rearrange("p j u n -> p j n u")
-            return woven1[first][:].bitcast(dtype).rearrange("p (j n) u -> p j n u", j=2), source
+        late0 = held.tile([P, Q, 2], U32, name="lower0", align_bytes=64)
+
+        def weave(dst, source):
+            nc.vector.tensor_copy(dst.bitcast(I32), source.rearrange("p u n e -> p u (n e)").bitcast(I32).rearrange("p u n -> p n u"))
+
+        weave(late0[:], upper0[:, 0])
 
         codes = {}
         scales = {}
@@ -149,7 +144,10 @@ def tile_moe_shr_lin_relu2_kernel(tc, xT, w_words, w_scales, b, gate, offs, out)
         def quantize(a, first, count):
             if a == 0:
                 code = codes0[:, first : first + count]
-                values = woven0[:, first : first + count].rearrange("p n u e -> p (n u e)")
+                if first == HALF:
+                    values = late0[:].rearrange("p n u -> p (n u)").bitcast(BF16)
+                else:
+                    values = woven0[:, first : first + count].rearrange("p n u e -> p (n u e)")
             else:
                 code = held.tile([P, count], U32, name=f"codes1_{first}", align_bytes=64)[:]
                 values = woven1[first][:].rearrange("p n u -> p (n u)").bitcast(BF16)
@@ -160,13 +158,13 @@ def tile_moe_shr_lin_relu2_kernel(tc, xT, w_words, w_scales, b, gate, offs, out)
                     codes[a, first + at, width] = code[:, at : at + width]
                     scales[a, first + at, width] = scale[:, at : at + width]
 
-        nc.vector.tensor_copy(*upper_words(3 * Q, I32))
-        nc.scalar.copy(*upper_words(HALF, U32))
+        weave(woven1[3 * Q][:], upper1[:, 1])
         quantize(0, 3 * Q, Q)
         quantize(1, 3 * Q, Q)
         quantize(0, HALF, Q)
+        weave(woven1[HALF][:], upper1[:, 0])
         quantize(0, 0, HALF)
-        nc.vector.tensor_copy(woven1[0][:].bitcast(I32), lower1[:].rearrange("p u n e -> p u (n e)").bitcast(I32).rearrange("p u n -> p n u"))
+        weave(woven1[0][:], lower1[:])
         quantize(1, HALF, Q)
         quantize(1, 0, HALF)
 

@@ -81,7 +81,8 @@ def tile_moe_shr_lin_relu2_kernel(tc, xT, w_words, w_scales, b, gate, offs, out)
         for i in range(1, 4 * A):
             load_row(i // 4, i % 4)
         load_scales(4, 5)
-        load_w(6, 3)
+        load_w(6, 2)
+        load_w(8, 1)
         load_w(4, 2)
         nc.sync.dma_start(gates[1][:], gate[0:P, HALF:T])
         load_scales(0, 4)
@@ -257,25 +258,42 @@ def tile_moe_shr_lin_relu2_kernel(tc, xT, w_words, w_scales, b, gate, offs, out)
                     windows[h] = held.tile([P, T], F32, name=f"window{h}", align_bytes=64)
                     scatter(0, h)
                 continue
-            routed = held.tile([P, 2, Q], F32, name=f"routed{q}", align_bytes=64)
-            shared = held.tile([P, 2, Q], F32, name=f"shared{q}", align_bytes=64)
-            squares_on_scalar(banks["routed", q], jobs["routed", q], f"r_routed{q}", routed[:].rearrange("p h c -> p (h c)"))
-            squares_on_vector(q, (1, 0), held.tile([P, 2, Q], F32, name=f"r_shared{q}", align_bytes=64), shared)
             if q < last:
+                routed = held.tile([P, 2, Q], F32, name=f"routed{q}", align_bytes=64)
+                shared = held.tile([P, 2, Q], F32, name=f"shared{q}", align_bytes=64)
+                squares_on_scalar(banks["routed", q], jobs["routed", q], f"r_routed{q}", routed[:].rearrange("p h c -> p (h c)"))
+                squares_on_vector(q, (1, 0), held.tile([P, 2, Q], F32, name=f"r_shared{q}", align_bytes=64), shared)
                 gated = held.tile([P, 2, Q], F32, name="woven1_0" if q == 0 else f"gated{q}", align_bytes=64)
                 nc.gpsimd.tensor_tensor(gated[:], routed[:], weights(q).unsqueeze(1).to_broadcast([P, 2, Q]), MULT)
                 nc.gpsimd.tensor_tensor(sums[q][:], gated[:], shared[:], ADD)
-            else:
-                gated = held.tile([P, Q], F32, name="gated_last", align_bytes=64)
-                nc.gpsimd.tensor_tensor(gated[:], routed[:, 1, :], weights(q), MULT)
-                nc.gpsimd.tensor_tensor(sums[q][:, 1, :], gated[:], shared[:, 1, :], ADD)
-                gated = held.tile([P, Q], F32, name="gated_last", align_bytes=64)
-                nc.gpsimd.tensor_tensor(gated[:], routed[:, 0, :], weights(q), MULT)
 
-        for q in range(1, last):
-            for h in range(2):
-                scatter(q, h)
+        r = held.tile([P, 2, Q], F32, name="r_routed_last", align_bytes=64)
+        for i in (2, 3, 0, 1):
+            e, h = jobs["routed", last][i][:2]
+            nc.scalar.activation(r[:, h, C * (i % 2) : C * (i % 2) + C], banks["routed", last][:, C * i : C * i + C], RELU, bias=bias[:, h, e : e + 1])
+        routed = held.tile([P, Q], F32, name="routed_last", align_bytes=64)
+        nc.scalar.activation(routed[:], r[:, 1, :], SQUARE)
+        bank = banks["shared", last]
+        shift = [bias[:, h, E : E + 1] for h in range(2)]
+        r_shared = held.tile([P, 2, Q], F32, name="r_shared_last", align_bytes=64)
+        for h in (1, 0):
+            nc.vector.tensor_scalar(r_shared[:, h, :], bank[:, Q * h : Q * h + Q], shift[h], 0.0, ADD, MAX)
+        shared = held.tile([P, Q], F32, name="shared_last", align_bytes=64)
+        nc.vector.scalar_tensor_tensor(shared[:], bank[:, Q : 2 * Q], shift[1], r_shared[:, 1, :], ADD, MULT)
+        gated = held.tile([P, Q], F32, name="gated_last", align_bytes=64)
+        nc.gpsimd.tensor_tensor(gated[:], routed[:], weights(last), MULT)
+        nc.gpsimd.tensor_tensor(sums[last][:, 1, :], gated[:], shared[:], ADD)
+        for h in range(2):
+            scatter(1, h)
+        routed = held.tile([P, Q], F32, name="routed_last0", align_bytes=64)
+        nc.scalar.activation(routed[:], r[:, 0, :], SQUARE)
+        shared = held.tile([P, Q], F32, name="shared_last0", align_bytes=64)
+        nc.vector.scalar_tensor_tensor(shared[:], bank[:, 0:Q], shift[0], r_shared[:, 0, :], ADD, MULT)
+        gated = held.tile([P, Q], F32, name="gated_last", align_bytes=64)
+        nc.gpsimd.tensor_tensor(gated[:], routed[:], weights(last), MULT)
+        for h in range(2):
+            scatter(split, h)
         scatter(last, 1)
-        nc.vector.tensor_tensor(place_of(last, 0), gated[:], shared[:, 0, :], ADD)
+        nc.vector.tensor_tensor(place_of(last, 0), gated[:], shared[:], ADD)
         for h in (1, 0):
             nc.sync.dma_start(out[P * h : P * h + P, :], windows[h][:])

@@ -42,9 +42,14 @@ def tile_moe_shr_lin_relu2_kernel(tc, xT, w_words, w_scales, b, gate, offs, out)
         w_at = {}
         s_at = {}
         planes = {}
+        zeros = held.tile([P, 4 * A, N // 4], U32, name="zeros", align_bytes=64)
+        nc.gpsimd.memset(zeros[:], 0)
         for first, count in ((4, 5), (0, 4)):
             planes[first] = held.tile([P, count * A, N], U8, name=f"planes{first}", align_bytes=64)
-            nc.gpsimd.memset(planes[first][:].bitcast(I32), 0)
+            if first:
+                nc.gpsimd.memset(planes[first][:].bitcast(I32), 0)
+            else:
+                nc.scalar.copy(planes[first][:].bitcast(U32), zeros[:])
             for i in range(count):
                 s_at[first + i] = (planes[first], i * A)
 
@@ -75,13 +80,13 @@ def tile_moe_shr_lin_relu2_kernel(tc, xT, w_words, w_scales, b, gate, offs, out)
         bias = held.tile([P, 2, 16], F32, name="bias")
         gates = [held.tile([P, HALF], F32, name=f"gates{i}") for i in range(2)]
 
-        nc.scalar.dma_start(bias[:, :, 0 : E + 1], b.rearrange("(h p) e -> p h e", p=P))
         load_row(0, 0)
         nc.sync.dma_start(offsets[:], offs)
         for i in range(1, 4 * A):
             load_row(i // 4, i % 4)
         load_scales(4, 5)
         load_w(6, 2)
+        nc.sync.dma_start(bias[:, :, 0 : E + 1], b.rearrange("(h p) e -> p h e", p=P))
         load_w(8, 1)
         load_w(4, 2)
         nc.sync.dma_start(gates[1][:], gate[0:P, HALF:T])
@@ -105,7 +110,7 @@ def tile_moe_shr_lin_relu2_kernel(tc, xT, w_words, w_scales, b, gate, offs, out)
             nc.scalar.activation(dst, picked(a, t, first, count), COPY)
 
         upper0 = held.tile([P, 2, 2, Q, 2], BF16, name="upper0", align_bytes=64)
-        lower0 = held.tile([P, 2, HALF, 2], BF16, name="lower0", align_bytes=64)
+        lower0 = held.tile([P, 4, HALF], BF16, name="lower0", align_bytes=64)
         for t in range(4):
             u, e = t // 2, t % 2
             if t < 3:
@@ -113,10 +118,13 @@ def tile_moe_shr_lin_relu2_kernel(tc, xT, w_words, w_scales, b, gate, offs, out)
             else:
                 for q in range(2):
                     on_vector(upper0[:, 1 - q, u, :, e], 0, t, firsts[q], Q)
-            on_scalar(lower0[:, u, :, e], 0, t, 0, HALF)
+            on_scalar(lower0[:, t, :], 0, t, 0, HALF)
         woven0 = held.tile([P, T, 2, 2], BF16, name="woven0", align_bytes=64)
-        for source, first in ((upper0[:, 1], 3 * Q), (lower0[:, :, Q:HALF, :], Q), (lower0[:, :, 0:Q, :], 0)):
-            nc.gpsimd.tensor_scalar(woven0[:, first : first + Q], source.rearrange("p u n e -> p n u e"), 1.0, 0.0, MULT, ADD)
+        nc.gpsimd.tensor_scalar(woven0[:, 3 * Q : T], upper0[:, 1].rearrange("p u n e -> p n u e"), 1.0, 0.0, MULT, ADD)
+        for first in (Q, 0):
+            nc.gpsimd.tensor_scalar(
+                woven0[:, first : first + Q].rearrange("p n u e -> p n (u e)"), lower0[:, :, first : first + Q].rearrange("p t n -> p n t"), 1.0, 0.0, MULT, ADD
+            )
 
         upper1 = held.tile([P, 2, 2, Q, 2], BF16, name="upper1", align_bytes=64)
         lower1 = held.tile([P, 2, HALF, 2], BF16, name="lower1", align_bytes=64)

@@ -121,10 +121,7 @@ def tile_moe_shr_lin_relu2_kernel(tc, xT, w_words, w_scales, b, gate, offs, out)
             on_scalar(lower0[:, t, :], 0, t, 0, HALF)
         woven0 = held.tile([P, T, 2, 2], BF16, name="woven0", align_bytes=64)
         nc.gpsimd.tensor_scalar(woven0[:, 3 * Q : T], upper0[:, 1].rearrange("p u n e -> p n u e"), 1.0, 0.0, MULT, ADD)
-        for first in (Q, 0):
-            nc.gpsimd.tensor_scalar(
-                woven0[:, first : first + Q].rearrange("p n u e -> p n (u e)"), lower0[:, :, first : first + Q].rearrange("p t n -> p n t"), 1.0, 0.0, MULT, ADD
-            )
+        nc.gpsimd.tensor_scalar(woven0[:, 0:HALF].rearrange("p n u e -> p n (u e)"), lower0[:].rearrange("p t n -> p n t"), 1.0, 0.0, MULT, ADD)
 
         upper1 = held.tile([P, 2, 2, Q, 2], BF16, name="upper1", align_bytes=64)
         lower1 = held.tile([P, 2, HALF, 2], BF16, name="lower1", align_bytes=64)
@@ -185,8 +182,8 @@ def tile_moe_shr_lin_relu2_kernel(tc, xT, w_words, w_scales, b, gate, offs, out)
         by_half = [jobs["routed", split][2 * h : 2 * h + 2] + [jobs["shared", split][h]] for h in range(2)]
         jobs["routed", split], jobs["shared", split] = by_half[1], by_half[0]
 
-        def passes(a, kind, q):
-            if a == 0:
+        def passes(a, kind, q, opens):
+            if opens:
                 banks[kind, q] = psum.tile([P, 2 * Q], F32, name=f"{kind}{q}")
             col = 0
             for i, (e, h, first, count) in enumerate(jobs[kind, q]):
@@ -198,15 +195,16 @@ def tile_moe_shr_lin_relu2_kernel(tc, xT, w_words, w_scales, b, gate, offs, out)
                     lhsT_scale=plane[:, at_s + a, P * h : P * h + P],
                     rhs=codes[a, first, count].bitcast(FP8X4),
                     rhs_scale=scales[a, first, count],
-                    start=(a == 0 and i == 0),
-                    stop=(a == A - 1 and i == len(jobs[kind, q]) - 1),
+                    start=(opens and i == 0),
+                    stop=(not opens and i == len(jobs[kind, q]) - 1),
                 )
                 col = col + count
 
         for q in range(NQ):
             for kind in ("routed", "shared"):
-                for a in range(A):
-                    passes(a, kind, q)
+                order = (1, 0) if (kind, q) == ("shared", 0) or q >= split else (0, 1)
+                for a in order:
+                    passes(a, kind, q, a == order[0])
 
         def squares_on_scalar(bank, parts, r_name, sq):
             r = held.tile([P, sq.shape[1]], F32, name=r_name, align_bytes=64)

@@ -37,7 +37,7 @@ def tile_moe_shr_lin_relu2_kernel(tc, xT, w_words, w_scales, b, gate, offs, out)
 
         offsets = held.tile([P, T // 16], U16, name="offsets")
 
-        firsts = [T - Q * (q + 1) for q in range(NQ)]
+        firsts = [2 * Q, 3 * Q, 0, Q]
 
         w_at = {}
         s_at = {}
@@ -85,15 +85,15 @@ def tile_moe_shr_lin_relu2_kernel(tc, xT, w_words, w_scales, b, gate, offs, out)
         for i in range(1, 4 * A):
             load_row(i // 4, i % 4)
         load_scales(4, 5)
-        load_w(6, 2)
+        load_w(4, 2)
         nc.sync.dma_start(bias[:, :, 0 : E + 1], b.rearrange("(h p) e -> p h e", p=P))
         load_w(8, 1)
-        load_w(4, 2)
+        load_w(6, 2)
         nc.sync.dma_start(gates[1][:], gate[0:P, HALF:T])
         load_scales(0, 4)
-        load_w(2, 2)
-        nc.sync.dma_start(gates[0][:], gate[0:P, 0:HALF])
         load_w(0, 2)
+        nc.sync.dma_start(gates[0][:], gate[0:P, 0:HALF])
+        load_w(2, 2)
 
         split = 2
         last = NQ - 1
@@ -117,31 +117,36 @@ def tile_moe_shr_lin_relu2_kernel(tc, xT, w_words, w_scales, b, gate, offs, out)
                 on_vector(upper0[:, :, u, :, e], 0, t, HALF, HALF)
             else:
                 for q in range(2):
-                    on_vector(upper0[:, 1 - q, u, :, e], 0, t, firsts[q], Q)
+                    on_vector(upper0[:, q, u, :, e], 0, t, firsts[q], Q)
             on_scalar(lower0[:, t, :], 0, t, 0, HALF)
         woven0 = held.tile([P, T, 2, 2], BF16, name="woven0", align_bytes=64)
-        nc.gpsimd.tensor_scalar(woven0[:, 3 * Q : T], upper0[:, 1].rearrange("p u n e -> p n u e"), 1.0, 0.0, MULT, ADD)
+        nc.gpsimd.tensor_scalar(woven0[:, HALF : 3 * Q], upper0[:, 0].rearrange("p u n e -> p n u e"), 1.0, 0.0, MULT, ADD)
         nc.gpsimd.tensor_scalar(woven0[:, 0:HALF].rearrange("p n u e -> p n (u e)"), lower0[:].rearrange("p t n -> p n t"), 1.0, 0.0, MULT, ADD)
 
-        upper1 = held.tile([P, 2, 2, Q, 2], BF16, name="upper1", align_bytes=64)
+        upper1 = held.tile([P, 2, HALF, 2], BF16, name="upper1", align_bytes=64)
+        own = Q
         lower1 = held.tile([P, 2, HALF, 2], BF16, name="lower1", align_bytes=64)
         for t in range(4):
             u, e = t // 2, t % 2
             if t < 2:
-                on_vector(upper1[:, :, u, :, e], 1, t, HALF, HALF)
+                on_vector(upper1[:, u, :, e], 1, t, HALF, HALF)
             else:
-                on_vector(upper1[:, 1, u, :, e], 1, t, 3 * Q, Q)
-                on_scalar(upper1[:, 0, u, :, e], 1, t, HALF, Q)
-            on_scalar(lower1[:, u, :, e], 1, t, 0, HALF)
+                on_vector(upper1[:, u, 0:own, e], 1, t, HALF, own)
+                on_scalar(upper1[:, u, own:HALF, e], 1, t, HALF + own, HALF - own)
+            if t < 3:
+                on_scalar(lower1[:, u, :, e], 1, t, 0, HALF)
+            else:
+                for first in (0, Q):
+                    on_scalar(lower1[:, u, first : first + Q, e], 1, t, first, Q)
 
-        woven1 = {first: held.tile([P, count, 2], U32, name=f"woven1_{first}", align_bytes=64) for first, count in ((3 * Q, Q), (HALF, Q), (0, HALF))}
+        woven1 = {first: held.tile([P, count, 2], U32, name=f"woven1_{first}", align_bytes=64) for first, count in ((3 * Q, Q), (HALF, Q), (Q, Q), (0, Q))}
 
         late0 = held.tile([P, Q, 2], U32, name="lower0", align_bytes=64)
 
         def weave(dst, source):
             nc.vector.tensor_copy(dst.bitcast(I32), source.rearrange("p u n e -> p u (n e)").bitcast(I32).rearrange("p u n -> p n u"))
 
-        weave(late0[:], upper0[:, 0])
+        weave(late0[:], upper0[:, 1])
 
         codes = {}
         scales = {}
@@ -150,7 +155,7 @@ def tile_moe_shr_lin_relu2_kernel(tc, xT, w_words, w_scales, b, gate, offs, out)
         def quantize(a, first, count):
             if a == 0:
                 code = codes0[:, first : first + count]
-                if first == HALF:
+                if first == 3 * Q:
                     values = late0[:].rearrange("p n u -> p (n u)").bitcast(BF16)
                 else:
                     values = woven0[:, first : first + count].rearrange("p n u e -> p (n u e)")
@@ -164,15 +169,17 @@ def tile_moe_shr_lin_relu2_kernel(tc, xT, w_words, w_scales, b, gate, offs, out)
                     codes[a, first + at, width] = code[:, at : at + width]
                     scales[a, first + at, width] = scale[:, at : at + width]
 
-        weave(woven1[3 * Q][:], upper1[:, 1])
-        quantize(0, 3 * Q, Q)
-        quantize(1, 3 * Q, Q)
+        weave(woven1[HALF][:], upper1[:, :, 0:Q, :])
         quantize(0, HALF, Q)
-        weave(woven1[HALF][:], upper1[:, 0])
-        quantize(0, 0, HALF)
-        weave(woven1[0][:], lower1[:])
         quantize(1, HALF, Q)
-        quantize(1, 0, HALF)
+        quantize(0, 3 * Q, Q)
+        weave(woven1[3 * Q][:], upper1[:, :, Q:HALF, :])
+        quantize(0, 0, HALF)
+        quantize(1, 3 * Q, Q)
+        for first in (0, Q):
+            weave(woven1[first][:], lower1[:, :, first : first + Q, :])
+        for first in (0, Q):
+            quantize(1, first, Q)
 
         banks = {}
         jobs = {}
@@ -260,16 +267,15 @@ def tile_moe_shr_lin_relu2_kernel(tc, xT, w_words, w_scales, b, gate, offs, out)
                 half_on_vector(q, parts[:, 0, :], parts[:, 2, :])
                 nc.gpsimd.tensor_tensor(parts[:, 1, :], parts[:, 3, :], weights(q), MULT)
                 nc.gpsimd.tensor_tensor(sums[q][:], parts[:, 0:2, :], parts[:, 2:5:2, :], ADD)
-                for h in range(2):
-                    windows[h] = held.tile([P, T], F32, name=f"window{h}", align_bytes=64)
-                    scatter(0, h)
+                windows[0] = held.tile([P, T], F32, name="window0", align_bytes=64)
+                scatter(0, 0)
                 continue
             if q < last:
                 routed = held.tile([P, 2, Q], F32, name=f"routed{q}", align_bytes=64)
                 shared = held.tile([P, 2, Q], F32, name=f"shared{q}", align_bytes=64)
                 squares_on_scalar(banks["routed", q], jobs["routed", q], f"r_routed{q}", routed[:].rearrange("p h c -> p (h c)"))
                 squares_on_vector(q, (1, 0), held.tile([P, 2, Q], F32, name=f"r_shared{q}", align_bytes=64), shared)
-                gated = held.tile([P, 2, Q], F32, name="woven1_0" if q == 0 else f"gated{q}", align_bytes=64)
+                gated = held.tile([P, 2, Q], F32, name=f"woven1_{Q}" if q == 0 else f"gated{q}", align_bytes=64)
                 nc.gpsimd.tensor_tensor(gated[:], routed[:], weights(q).unsqueeze(1).to_broadcast([P, 2, Q]), MULT)
                 nc.gpsimd.tensor_tensor(sums[q][:], gated[:], shared[:], ADD)
 
@@ -277,6 +283,8 @@ def tile_moe_shr_lin_relu2_kernel(tc, xT, w_words, w_scales, b, gate, offs, out)
         for i in (2, 3, 0, 1):
             e, h = jobs["routed", last][i][:2]
             nc.scalar.activation(r[:, h, C * (i % 2) : C * (i % 2) + C], banks["routed", last][:, C * i : C * i + C], RELU, bias=bias[:, h, e : e + 1])
+        windows[1] = held.tile([P, T], F32, name="window1", align_bytes=64)
+        scatter(0, 1)
         routed = held.tile([P, Q], F32, name="routed_last", align_bytes=64)
         nc.scalar.activation(routed[:], r[:, 1, :], SQUARE)
         bank = banks["shared", last]

from contextlib import ExitStack

import concourse.mybir as mybir

K, T, E, C, N = 1024, 1024, 8, 128, 256
FLOPS = 2 * 2 * K * T * N

F32 = mybir.dt.float32
BF16 = mybir.dt.bfloat16
U32 = mybir.dt.uint32
I32 = mybir.dt.int32
U16 = mybir.dt.uint16
U8 = mybir.dt.uint8
FP8X4 = mybir.dt.float8_e4m3fn_x4
FP4X4 = mybir.dt.float4_e2m1fn_x4

ADD = mybir.AluOpType.add
MULT = mybir.AluOpType.mult
MAX = mybir.AluOpType.max
IS_GT = mybir.AluOpType.is_gt
RELU = mybir.ActivationFunctionType.Relu
SQUARE = mybir.ActivationFunctionType.Square
COPY = mybir.ActivationFunctionType.Copy

P = 128
A = K // 512
Q = 256
NQ = T // Q
HALF = T // 2


def tile_moe_shr_lin_relu2_kernel(tc, xT, w_words, w_scales, b, gate, offs, out):
    nc = tc.nc
    with ExitStack() as ctx:
        held = ctx.enter_context(tc.tile_pool(name="held", bufs=1))
        psum = ctx.enter_context(tc.psum_pool(name="psum", bufs=1))

        offsets = held.tile([P, T // 16], U16, name="offsets")

        firsts = [2 * Q, 3 * Q, 0, Q]

        w_at = {}
        s_at = {}
        planes = {}
        zeros = held.tile([P, 4 * A, N // 4], U32, name="zeros", align_bytes=64)
        nc.gpsimd.memset(zeros[:], 0)
        for first, count in ((4, 5), (0, 4)):
            planes[first] = held.tile([P, count * A, N], U8, name=f"planes{first}", align_bytes=64)
            if first:
                nc.gpsimd.memset(planes[first][:].bitcast(I32), 0)
            else:
                nc.scalar.copy(planes[first][:].bitcast(U32), zeros[:])
            for i in range(count):
                s_at[first + i] = (planes[first], i * A)

        x_rows = xT.rearrange("(a p t) n -> a t p n", p=P, t=4)
        rows = {}

        def load_row(a, t):
            row = held.tile([P, T], F32, name=f"row{a}{t}", align_bytes=64)
            nc.sync.dma_start(row[:], x_rows[a, t])
            rows[a, t] = row

        w_view = w_words.bitcast(I32)
        s_view = w_scales.bitcast(I32)

        def load_w(first, count):
            tile = held.tile([P, count * A, 2 * N], U8, name=f"words{first}", align_bytes=64)
            nc.sync.dma_start(tile[:].bitcast(I32), w_view[first : first + count].rearrange("e a p c -> p (e a) c"))
            for i in range(count):
                w_at[first + i] = (tile, i * A)

        def load_scales(first, count):
            for r in range(4):
                nc.sync.dma_start(
                    planes[first][r:P:32].bitcast(I32),
                    s_view[first : first + count, :, r:16:4, :].rearrange("e a q n -> q (e a) n"),
                )

        bias = held.tile([P, 2, 16], F32, name="bias")
        gates = [held.tile([P, HALF], F32, name=f"gates{i}") for i in range(2)]

        load_row(0, 0)
        nc.sync.dma_start(offsets[:], offs)
        for i in range(1, 4 * A):
            load_row(i // 4, i % 4)
        load_scales(4, 5)
        load_w(4, 2)
        nc.sync.dma_start(bias[:, :, 0 : E + 1], b.rearrange("(h p) e -> p h e", p=P))
        load_w(8, 1)
        load_w(6, 2)
        nc.sync.dma_start(gates[1][:], gate[0:P, HALF:T])
        load_scales(0, 4)
        load_w(0, 2)
        nc.sync.dma_start(gates[0][:], gate[0:P, 0:HALF])
        load_w(2, 2)

        split = 2
        last = NQ - 1
        minus_bias = held.tile([P, 2], F32, name="minus_bias")
        nc.scalar.activation(minus_bias[:], bias[:, 0, firsts[split] // C : firsts[split] // C + 2], COPY, scale=-1.0)

        def picked(a, t, first, count):
            return rows[a, t][:].indirect(offsets[:, first // 16 : (first + count) // 16])

        def on_vector(dst, a, t, first, count):
            nc.vector.tensor_copy(dst, picked(a, t, first, count))

        def on_scalar(dst, a, t, first, count):
            nc.scalar.activation(dst, picked(a, t, first, count), COPY)

        upper0 = held.tile([P, 2, 2, Q, 2], BF16, name="upper0", align_bytes=64)
        lower0 = held.tile([P, 4, HALF], BF16, name="lower0", align_bytes=64)
        for t in range(4):
            u, e = t // 2, t % 2
            if t < 3:
                on_vector(upper0[:, :, u, :, e], 0, t, HALF, HALF)
            else:
                for q in range(2):
                    on_vector(upper0[:, q, u, :, e], 0, t, firsts[q], Q)
            on_scalar(lower0[:, t, :], 0, t, 0, HALF)
        woven0 = held.tile([P, T, 2, 2], BF16, name="woven0", align_bytes=64)
        nc.gpsimd.tensor_scalar(woven0[:, HALF : 3 * Q], upper0[:, 0].rearrange("p u n e -> p n u e"), 1.0, 0.0, MULT, ADD)
        nc.gpsimd.tensor_scalar(woven0[:, 0:HALF].rearrange("p n u e -> p n (u e)"), lower0[:].rearrange("p t n -> p n t"), 1.0, 0.0, MULT, ADD)

        upper1 = held.tile([P, 2, HALF, 2], BF16, name="upper1", align_bytes=64)
        own = Q
        lower1 = held.tile([P, 2, HALF, 2], BF16, name="lower1", align_bytes=64)
        for t in range(4):
            u, e = t // 2, t % 2
            if t < 2:
                on_vector(upper1[:, u, :, e], 1, t, HALF, HALF)
            else:
                on_vector(upper1[:, u, 0:own, e], 1, t, HALF, own)
                on_scalar(upper1[:, u, own:HALF, e], 1, t, HALF + own, HALF - own)
            if t < 3:
                on_scalar(lower1[:, u, :, e], 1, t, 0, HALF)
            else:
                for first in (0, Q):
                    on_scalar(lower1[:, u, first : first + Q, e], 1, t, first, Q)

        woven1 = {first: held.tile([P, count, 2], U32, name=f"woven1_{first}", align_bytes=64) for first, count in ((3 * Q, Q), (HALF, Q), (Q, Q), (0, Q))}

        late0 = held.tile([P, Q, 2], U32, name="lower0", align_bytes=64)

        def weave(dst, source):
            nc.vector.tensor_copy(dst.bitcast(I32), source.rearrange("p u n e -> p u (n e)").bitcast(I32).rearrange("p u n -> p n u"))

        weave(late0[:], upper0[:, 1])

        codes = {}
        scales = {}
        codes0 = held.tile([P, T], U32, name="upper0", align_bytes=64)

        def quantize(a, first, count):
            if a == 0:
                code = codes0[:, first : first + count]
                if first == 3 * Q:
                    values = late0[:].rearrange("p n u -> p (n u)").bitcast(BF16)
                else:
                    values = woven0[:, first : first + count].rearrange("p n u e -> p (n u e)")
            else:
                code = held.tile([P, count], U32, name=f"codes1_{first}", align_bytes=64)[:]
                values = woven1[first][:].rearrange("p n u -> p (n u)").bitcast(BF16)
            scale = held.tile([P, count], U8, name=f"scales{a}_{first}", align_bytes=64)
            nc.vector.quantize_mx(out=code.bitcast(FP8X4), scales=scale[:], in_=values)
            for width in (C, Q):
                for at in range(0, count, width):
                    codes[a, first + at, width] = code[:, at : at + width]
                    scales[a, first + at, width] = scale[:, at : at + width]

        weave(woven1[HALF][:], upper1[:, :, 0:Q, :])
        quantize(0, HALF, Q)
        quantize(1, HALF, Q)
        quantize(0, 3 * Q, Q)
        weave(woven1[3 * Q][:], upper1[:, :, Q:HALF, :])
        quantize(0, 0, HALF)
        quantize(1, 3 * Q, Q)
        for first in (0, Q):
            weave(woven1[first][:], lower1[:, :, first : first + Q, :])
        for first in (0, Q):
            quantize(1, first, Q)

        banks = {}
        jobs = {}
        for q in range(NQ):
            jobs["routed", q] = [(firsts[q] // C + j, h, firsts[q] + C * j, C) for h in range(2) for j in range(2)]
            jobs["shared", q] = [(E, h, firsts[q], Q) for h in range(2)]
        by_half = [jobs["routed", split][2 * h : 2 * h + 2] + [jobs["shared", split][h]] for h in range(2)]
        jobs["routed", split], jobs["shared", split] = by_half[1], by_half[0]

        def passes(a, kind, q, opens):
            if opens:
                banks[kind, q] = psum.tile([P, 2 * Q], F32, name=f"{kind}{q}")
            col = 0
            for i, (e, h, first, count) in enumerate(jobs[kind, q]):
                words, at = w_at[e]
                plane, at_s = s_at[e]
                nc.tensor.matmul_mx(
                    out=banks[kind, q][:, col : col + count],
                    lhsT=words[:, at + a, N * h : N * h + N].bitcast(FP4X4),
                    lhsT_scale=plane[:, at_s + a, P * h : P * h + P],
                    rhs=codes[a, first, count].bitcast(FP8X4),
                    rhs_scale=scales[a, first, count],
                    start=(opens and i == 0),
                    stop=(not opens and i == len(jobs[kind, q]) - 1),
                )
                col = col + count

        for q in range(NQ):
            for kind in ("routed", "shared"):
                order = (1, 0) if (kind, q) == ("shared", 0) or q >= split else (0, 1)
                for a in order:
                    passes(a, kind, q, a == order[0])

        def squares_on_scalar(bank, parts, r_name, sq):
            r = held.tile([P, sq.shape[1]], F32, name=r_name, align_bytes=64)
            col = 0
            for e, h, first, count in parts:
                nc.scalar.activation(r[:, col : col + count], bank[:, col : col + count], RELU, bias=bias[:, h, e : e + 1])
                col = col + count
            nc.scalar.activation(sq, r[:], SQUARE)

        def squares_on_vector(q, halves, r, sq):
            bank = banks["shared", q]
            for h in halves:
                nc.vector.tensor_scalar(r[:, h, :], bank[:, Q * h : Q * h + Q], bias[:, h, E : E + 1], 0.0, ADD, MAX)
            for h in halves:
                nc.vector.scalar_tensor_tensor(sq[:, h, :], bank[:, Q * h : Q * h + Q], bias[:, h, E : E + 1], r[:, h, :], ADD, MULT)

        def weights(q):
            return gates[firsts[q] // HALF][:, firsts[q] % HALF : firsts[q] % HALF + Q]

        def half_on_vector(q, gated, shared):
            bank = banks["shared", q]
            e = firsts[q] // C

            def step(op0, shift, source, target):
                for j in range(2):
                    cols = slice(C * j, C * j + C)
                    nc.vector.scalar_tensor_tensor(target[:, cols], bank[:, cols], shift[:, j : j + 1], source[:, cols], op0, MULT)

            step(IS_GT, minus_bias[:], weights(q), steps[:, 0, :])
            nc.vector.tensor_scalar(steps[:, 2, :], bank[:, Q : 2 * Q], bias[:, 0, E : E + 1], 0.0, ADD, MAX)
            step(ADD, bias[:, 0, e : e + 2], steps[:, 0, :], steps[:, 1, :])
            nc.vector.scalar_tensor_tensor(shared, bank[:, Q : 2 * Q], bias[:, 0, E : E + 1], steps[:, 2, :], ADD, MULT)
            step(ADD, bias[:, 0, e : e + 2], steps[:, 1, :], gated)

        windows = {}
        sums = {}

        def place_of(q, h):
            return windows[h][:].indirect(offsets[:, firsts[q] // 16 : (firsts[q] + Q) // 16])

        def scatter(q, h):
            if h == 0:
                nc.vector.tensor_copy(place_of(q, 0), sums[q][:, 0, :])
            else:
                nc.scalar.activation(place_of(q, 1), sums[q][:, 1, :], COPY)

        for q in range(NQ):
            sums[q] = held.tile([P, 2, Q], F32, name=f"sums{q}", align_bytes=64)
            if q == split:
                parts = held.tile([P, 5, Q], F32, name="parts", align_bytes=64)
                steps = held.tile([P, 3, Q], F32, name="window0", align_bytes=64)
                squares_on_scalar(banks["routed", q], jobs["routed", q], "window1", parts[:, 3:5, :].rearrange("p j c -> p (j c)"))
                half_on_vector(q, parts[:, 0, :], parts[:, 2, :])
                nc.gpsimd.tensor_tensor(parts[:, 1, :], parts[:, 3, :], weights(q), MULT)
                nc.gpsimd.tensor_tensor(sums[q][:], parts[:, 0:2, :], parts[:, 2:5:2, :], ADD)
                windows[0] = held.tile([P, T], F32, name="window0", align_bytes=64)
                scatter(0, 0)
                continue
            if q < last:
                routed = held.tile([P, 2, Q], F32, name=f"routed{q}", align_bytes=64)
                shared = held.tile([P, 2, Q], F32, name=f"shared{q}", align_bytes=64)
                squares_on_scalar(banks["routed", q], jobs["routed", q], f"r_routed{q}", routed[:].rearrange("p h c -> p (h c)"))
                squares_on_vector(q, (1, 0), held.tile([P, 2, Q], F32, name=f"r_shared{q}", align_bytes=64), shared)
                gated = held.tile([P, 2, Q], F32, name=f"woven1_{Q}" if q == 0 else f"gated{q}", align_bytes=64)
                nc.gpsimd.tensor_tensor(gated[:], routed[:], weights(q).unsqueeze(1).to_broadcast([P, 2, Q]), MULT)
                nc.gpsimd.tensor_tensor(sums[q][:], gated[:], shared[:], ADD)

        r = held.tile([P, 2, Q], F32, name="r_routed_last", align_bytes=64)
        for i in (2, 3, 0, 1):
            e, h = jobs["routed", last][i][:2]
            nc.scalar.activation(r[:, h, C * (i % 2) : C * (i % 2) + C], banks["routed", last][:, C * i : C * i + C], RELU, bias=bias[:, h, e : e + 1])
        windows[1] = held.tile([P, T], F32, name="window1", align_bytes=64)
        scatter(0, 1)
        routed = held.tile([P, Q], F32, name="routed_last", align_bytes=64)
        nc.scalar.activation(routed[:], r[:, 1, :], SQUARE)
        bank = banks["shared", last]
        shift = [bias[:, h, E : E + 1] for h in range(2)]
        r_shared = held.tile([P, 2, Q], F32, name="r_shared_last", align_bytes=64)
        for h in (1, 0):
            nc.vector.tensor_scalar(r_shared[:, h, :], bank[:, Q * h : Q * h + Q], shift[h], 0.0, ADD, MAX)
        shared = held.tile([P, Q], F32, name="shared_last", align_bytes=64)
        nc.vector.scalar_tensor_tensor(shared[:], bank[:, Q : 2 * Q], shift[1], r_shared[:, 1, :], ADD, MULT)
        gated = held.tile([P, Q], F32, name="gated_last", align_bytes=64)
        nc.gpsimd.tensor_tensor(gated[:], routed[:], weights(last), MULT)
        nc.gpsimd.tensor_tensor(sums[last][:, 1, :], gated[:], shared[:], ADD)
        for h in range(2):
            scatter(1, h)
        routed = held.tile([P, Q], F32, name="routed_last0", align_bytes=64)
        nc.scalar.activation(routed[:], r[:, 0, :], SQUARE)
        shared = held.tile([P, Q], F32, name="shared_last0", align_bytes=64)
        nc.vector.scalar_tensor_tensor(shared[:], bank[:, 0:Q], shift[0], r_shared[:, 0, :], ADD, MULT)
        gated = held.tile([P, Q], F32, name="gated_last", align_bytes=64)
        nc.gpsimd.tensor_tensor(gated[:], routed[:], weights(last), MULT)
        for h in range(2):
            scatter(split, h)
        scatter(last, 1)
        nc.vector.tensor_tensor(place_of(last, 0), gated[:], shared[:], ADD)
        for h in (1, 0):
            nc.sync.dma_start(out[P * h : P * h + P, :], windows[h][:])
